import numpy as np
import ml_dtypes


def mxq(x, axis, fmt="e4m3"):
    dtype, down = {"e4m3": (ml_dtypes.float8_e4m3fn, 7), "e5m2": (ml_dtypes.float8_e5m2, 14)}[fmt]
    v = np.moveaxis(np.asarray(x, np.float32).astype(ml_dtypes.bfloat16).astype(np.float64), axis, -1)
    blocks = v.reshape(v.shape[:-1] + (-1, 32))
    amax = np.abs(blocks).max(-1, keepdims=True)
    byte = np.maximum(np.where(amax > 0, np.frexp(amax)[1] - 1 + 127, 0) - down, 1)
    scale = np.exp2(byte - 127.0)
    codes = (blocks / scale).astype(np.float32).astype(dtype).astype(np.float64)
    return np.moveaxis((codes * scale).reshape(v.shape), -1, axis)


WIDE = False


def mx_kscale(k):
    if not WIDE:
        return np.ones(k)
    levels = np.array([10, -10, 5, -5, 0])
    if k % 512:
        return np.exp2(np.random.permutation(np.resize(levels, k // 32))).repeat(32)
    a = np.empty((k // 512, 16))
    for p in range(k // 512):
        a[p, :8] = np.random.permutation(np.resize(levels, 8))
        for g in range(8):
            far = levels[np.abs(levels - a[p, g]) >= 10]
            a[p, g + 8] = far[np.random.randint(len(far))]
    return np.exp2(a.ravel()).repeat(32)


BF16 = ml_dtypes.bfloat16


def bf(x):
    return np.asarray(x, np.float32).astype(BF16)


def f64(x):
    return np.asarray(x).astype(np.float64)


E2M1 = np.array([0.0, 0.5, 1.0, 1.5, 2.0, 3.0, 4.0, 6.0, -0.0, -0.5, -1.0, -1.5, -2.0, -3.0, -4.0, -6.0])


def pack_weight(w, fmt):
    k, n = w.shape
    w = f64(bf(w)).reshape(k // 32, 32, n)
    amax = np.abs(w).max(1)
    if fmt == "e4m3":
        byte = np.frexp(amax)[1] - 1 + 127 - 7
    else:
        mant, ex = np.frexp(amax / 6.0)
        byte = np.where(mant > 0.5, ex, ex - 1) + 127
    byte = np.clip(np.where(amax > 0, byte, 1), 1, 254)
    scaled = (w * np.exp2(127.0 - byte)[:, None, :]).reshape(k, n).astype(np.float32)
    by_word = np.ascontiguousarray(scaled.reshape(k // 512, 128, 4, n).transpose(0, 1, 3, 2))
    if fmt == "e4m3":
        words = by_word.astype(ml_dtypes.float8_e4m3fn).view(np.uint8)
    else:
        c = by_word.astype(ml_dtypes.float4_e2m1fn).view(np.uint8) & 0xF
        words = c[..., 0::2] | (c[..., 1::2] << 4)
    return np.ascontiguousarray(words), np.ascontiguousarray(byte.astype(np.uint8).reshape(k // 512, 16, n))


def unpack_weight(words, scales, fmt):
    g, p, n, _ = words.shape
    if fmt == "e4m3":
        vals = np.ascontiguousarray(words).view(ml_dtypes.float8_e4m3fn).astype(np.float64)
    else:
        nib = np.empty((g, p, n, 4), np.uint8)
        nib[..., 0::2] = words & 0xF
        nib[..., 1::2] = words >> 4
        vals = E2M1[nib]
    vals = vals * np.repeat(np.exp2(scales.astype(np.float64) - 127.0), 8, axis=1)[..., None]
    return vals.transpose(0, 1, 3, 2).reshape(g * 512, n)
def pack4(w):
    words, scales = pack_weight(w, "e2m1")
    return words.reshape(words.shape[0], 128, -1), scales


def unpack4(words, scales):
    return unpack_weight(words.reshape(words.shape[0], 128, -1, 2), scales, "e2m1")


M, KA, KB, N, D = 1024, 1024, 2048, 1024, 1536

STAB = 0.25


def draw0():
    sa, sb, t = mx_kscale(KA), mx_kscale(KB), mx_kscale(N)
    z = np.random.standard_normal((M, N))
    b_words, b_scales = pack4(np.random.standard_normal((KB, N)) / np.sqrt(KB) / sb[:, None])
    u_words, u_scales = pack4(np.random.standard_normal((N, D)) / np.sqrt(N) / t[:, None])
    return {"ra": bf(np.random.standard_normal((M, KA)) * sa),
            "a": bf(np.random.standard_normal((KA, N)) / np.sqrt(KA) / sa[:, None]),
            "rb": bf(np.random.standard_normal((M, KB)) * sb),
            "b_words": b_words, "b_scales": b_scales,
            "h": bf(z / (1 + np.exp(-z))),
            "d": bf((z + np.copysign(STAB, z)) / t),
            "x": bf(np.random.standard_normal((M, D))),
            "u_words": u_words, "u_scales": u_scales}


def core(ra, a, rb, b_words, b_scales, h, d, x, u_words, u_scales):
    ca = mxq(f64(ra), 1, "e4m3") @ mxq(f64(a), 0, "e4m3")
    cb = mxq(f64(rb), 1, "e4m3") @ unpack4(b_words, b_scales)
    rel_h = f64(h) * (ca + cb)
    f = rel_h / f64(d)
    back = mxq(f, 1, "e4m3") @ unpack4(u_words, u_scales)
    rel_x = f64(x) * back
    return rel_h, rel_x


def e4m3fn_bytes(y):
    return np.clip(np.asarray(y, np.float64), -448.0, 448.0).astype(np.float32).astype(ml_dtypes.float8_e4m3fn).view(np.uint8)


def e4m3fn_values(b):
    return np.asarray(b, np.uint8).view(ml_dtypes.float8_e4m3fn).astype(np.float64)


def setup_inputs():
    d = draw0()
    x0 = np.asarray(d['rb']).astype(np.float64)
    s = (np.max(np.abs(x0), axis=(0,), keepdims=True) / 448.0).astype(np.float32)
    out = {}
    for k, v in d.items():
        if k == 'rb':
            out['rb_bytes'] = e4m3fn_bytes(x0 / s.astype(np.float64))
            out['rb_scale'] = s
        else:
            out[k] = v
    return out


def reference(ra, a, rb_bytes, rb_scale, b_words, b_scales, h, d, x, u_words, u_scales):
    return core(ra, a, e4m3fn_values(rb_bytes) * rb_scale.astype(np.float64), b_words, b_scales, h, d, x, u_words, u_scales)

@@ -1,0 +1,322 @@
+from contextlib import ExitStack
+
+import concourse.mybir as mybir
+from concourse.masks import make_identity
+
+M, KA, KB, N, D = 1024, 1024, 2048, 1024, 1536
+FLOPS = 2 * M * (KA * N + KB * N + N * D)
+
+F32 = mybir.dt.float32
+BF16 = mybir.dt.bfloat16
+I32 = mybir.dt.int32
+U32 = mybir.dt.uint32
+U8 = mybir.dt.uint8
+FP8 = mybir.dt.float8_e4m3fn
+FP8X4 = mybir.dt.float8_e4m3fn_x4
+FP4X4 = mybir.dt.float4_e2m1fn_x4
+ALU = mybir.AluOpType
+ACT = mybir.ActivationFunctionType
+
+P = 128
+TILES = M // P
+GA, GB, GN = KA // 512, KB // 512, N // 512
+SIGN_BITS = -2147450880
+
+
+def tile_relevance_step_fanout_s3_kernel(
+    tc, ra, a, rb_bytes, rb_scale, b_words, b_scales, h, d, x, u_words, u_scales, rel_h, rel_x
+):
+    nc = tc.nc
+    with ExitStack() as ctx:
+        keep = ctx.enter_context(tc.tile_pool(name="keep", bufs=1))
+        stream = ctx.enter_context(tc.tile_pool(name="stream", bufs=3))
+        araw_pool = ctx.enter_context(tc.tile_pool(name="araw", bufs=2))
+        work = ctx.enter_context(tc.tile_pool(name="work", bufs=2))
+        wide = ctx.enter_context(tc.tile_pool(name="wide", bufs=4))
+        outs = ctx.enter_context(tc.tile_pool(name="outs", bufs=2))
+        c_psum = ctx.enter_context(tc.psum_pool(name="c_psum", bufs=2))
+        b_psum = ctx.enter_context(tc.psum_pool(name="b_psum", bufs=3))
+        t_psum = ctx.enter_context(tc.psum_pool(name="t_psum", bufs=3))
+        ctx.enter_context(tc.manual_schedule())
+
+        def row_view(t):
+            return t.rearrange("(p i) k -> p i k", i=TILES)
+
+        ra_v, rb_v, h_v, d_v, x_v = [row_view(t) for t in (ra, rb_bytes, h, d, x)]
+        rel_h_v, rel_x_v = row_view(rel_h), row_view(rel_x)
+        ra_sb, rb_sb, h_sb, d_sb, x_sb = {}, {}, {}, {}, {}
+
+        def load_pair(store, name, view, width, dtype, j):
+            t = stream.tile([P, 2, width], dtype, name=name, align_bytes=64)
+            nc.sync.dma_start(out=t[:], in_=view[:, 2 * j : 2 * j + 2, :])
+            store[j] = t
+
+        ident = keep.tile([P, P], F32, name="ident")
+        make_identity(nc, ident[:])
+        bsc = keep.tile([P, GB * N], U8, name="bsc", align_bytes=64)
+        usc = keep.tile([P, GN * D], U8, name="usc", align_bytes=64)
+        nc.gpsimd.memset(bsc[:].bitcast(I32), 0)
+        nc.gpsimd.memset(usc[:].bitcast(I32), 0)
+
+        scale_bc = [keep.tile([P, KB // 2], F32, name=f"scale_bc{k}", align_bytes=64) for k in range(2)]
+        a_raw = [araw_pool.tile([P, 4, N], BF16, name="a_raw", align_bytes=64) for g in range(GA)]
+
+        def load_scale(k):
+            half = rb_scale[:, k * KB // 2 : (k + 1) * KB // 2]
+            nc.sync.dma_start(out=scale_bc[k][:], in_=half.rearrange("o k -> (o k)").partition_broadcast(P))
+
+        def load_a(g):
+            nc.sync.dma_start(out=a_raw[g][:], in_=a[512 * g : 512 * (g + 1), :].rearrange("(p j) n -> p j n", j=4))
+
+        def load_rows(name, j):
+            store, view, width, dtype = {
+                "ra": (ra_sb, ra_v, KA, BF16),
+                "rb": (rb_sb, rb_v, KB, U8),
+                "h": (h_sb, h_v, N, BF16),
+                "d": (d_sb, d_v, N, BF16),
+                "x": (x_sb, x_v, D, BF16),
+            }[name]
+            load_pair(store, name + "_in", view, width, dtype, j)
+
+        b_sb = keep.tile([P, GB, 2 * N], U8, name="b_sb", align_bytes=64)
+        u_sb = keep.tile([P, GN, 2 * D], U8, name="u_sb", align_bytes=64)
+        load_scale(0)
+        load_rows("rb", 0)
+        load_scale(1)
+        load_rows("ra", 0)
+        load_a(0)
+        load_a(1)
+        for q in range(4):
+            nc.sync.dma_start(
+                out=bsc[32 * q : 32 * q + 4, :].bitcast(I32).rearrange("p (g n) -> p g n", g=GB),
+                in_=b_scales[:, 4 * q : 4 * q + 4, :].bitcast(I32).rearrange("g q n -> q g n"),
+            )
+        for q in range(4):
+            nc.sync.dma_start(
+                out=usc[32 * q : 32 * q + 4, :].bitcast(I32).rearrange("p (g n) -> p g n", g=GN),
+                in_=u_scales[:, 4 * q : 4 * q + 4, :].bitcast(I32).rearrange("g q n -> q g n"),
+            )
+        nc.sync.dma_start(out=b_sb[:], in_=b_words.rearrange("g p c -> p g c"))
+        load_rows("rb", 1)
+        load_rows("d", 0)
+        load_rows("h", 0)
+        load_rows("ra", 1)
+        nc.sync.dma_start(out=u_sb[:], in_=u_words.rearrange("g p c -> p g c"))
+        for name in ("d", "h"):
+            load_rows(name, 1)
+        load_rows("x", 0)
+        for name in ("rb", "ra", "d", "h"):
+            load_rows(name, 2)
+        load_rows("x", 1)
+
+        rbw, grp, codes, scls, sgn_h, wt, f_sb, f_codes, f_scls = {}, {}, {}, {}, {}, {}, {}, {}, {}
+        c_acc, x_acc, recip = {}, {}, {}
+
+        def widen(i, part):
+            if part == 0:
+                rbw[i] = wide.tile([P, KB], BF16, name="rbw", align_bytes=64)
+            cols = slice(part * KB // 2, (part + 1) * KB // 2)
+            nc.vector.tensor_tensor(
+                out=rbw[i][:, cols], in0=rb_sb[i // 2][:, i % 2, cols].bitcast(FP8), in1=scale_bc[part][:], op=ALU.mult
+            )
+
+        def transpose_bank(words, base, step, out_words):
+            xt = t_psum.tile([P, 2, 2, P], F32, name="xt")
+            for g in range(2):
+                for u in range(2):
+                    if step == 2:
+                        first = base + 256 * g + u
+                        src = words[:, first : first + 255 : 2]
+                    else:
+                        first = base + 256 * g + 128 * u
+                        src = words[:, first : first + 128]
+                    nc.tensor.transpose(xt[:, g, u, :], src, ident[:])
+            nc.scalar.copy(
+                out=out_words.rearrange("p (g r u) -> p g r u", g=2, u=2), in_=xt[:].rearrange("p g u r -> p g r u")
+            )
+
+        def turn_ra(i):
+            grp["ra", i] = work.tile([P, KA], BF16, name="ra_grp", align_bytes=64)
+            transpose_bank(ra_sb[i // 2][:, i % 2, :].bitcast(F32), 0, 2, grp["ra", i][:].bitcast(F32))
+
+        def turn_rb(i, half):
+            if half == 0:
+                grp["rb", i] = work.tile([P, KB], BF16, name="rb_grp", align_bytes=64)
+            transpose_bank(
+                rbw[i][:].bitcast(F32), 512 * half, 2, grp["rb", i][:, 1024 * half : 1024 * (half + 1)].bitcast(F32)
+            )
+
+        def quant(kind, i, width):
+            codes[kind, i] = work.tile([P, width // 4], U32, name=f"{kind}_codes", align_bytes=64)
+            scls[kind, i] = work.tile([P, width // 4], U8, name=f"{kind}_scls", align_bytes=64)
+            nc.vector.quantize_mx(out=codes[kind, i][:].bitcast(FP8X4), scales=scls[kind, i][:], in_=grp[kind, i][:])
+
+        def reciprocal_d(i):
+            dt = d_sb[i // 2][:, i % 2, :]
+            y = work.tile([P, N], F32, name="y")
+            nc.scalar.activation(out=y[:], in_=dt, func=ACT.Abs_reciprocal_sqrt)
+            nc.scalar.activation(out=y[:], in_=y[:], func=ACT.Square)
+            recip[i] = y
+
+        def weight_sign(i):
+            dt, ht = d_sb[i // 2][:, i % 2, :], h_sb[i // 2][:, i % 2, :]
+            sh = work.tile([P, N], BF16, name="sh")
+            nc.vector.scalar_tensor_tensor(
+                out=sh[:].bitcast(I32),
+                in0=dt.bitcast(I32),
+                scalar=SIGN_BITS,
+                in1=ht.bitcast(I32),
+                op0=ALU.bitwise_and,
+                op1=ALU.bitwise_xor,
+            )
+            wt[i] = work.tile([P, N], F32, name="wt")
+            nc.gpsimd.tensor_tensor(out=wt[i][:], in0=sh[:], in1=recip[i][:], op=ALU.mult)
+
+        def product_c(i, half):
+            acc = c_psum.tile([P, 512], F32, name="c_acc")
+            c_acc[half] = acc
+            cols = slice(512 * half, 512 * (half + 1))
+            for g in range(GB):
+                nc.tensor.matmul_mx(
+                    out=acc[:],
+                    lhsT=codes["rb", i][:, 128 * g : 128 * (g + 1)].bitcast(FP8X4),
+                    lhsT_scale=scls["rb", i][:, 128 * g : 128 * (g + 1)],
+                    rhs=b_sb[:, g, 1024 * half : 1024 * (half + 1)].bitcast(FP4X4),
+                    rhs_scale=bsc[:, N * g + 512 * half : N * g + 512 * (half + 1)],
+                    start=(g == 0),
+                    stop=False,
+                )
+            for g in range(GA):
+                nc.tensor.matmul_mx(
+                    out=acc[:],
+                    lhsT=codes["ra", i][:, 128 * g : 128 * (g + 1)].bitcast(FP8X4),
+                    lhsT_scale=scls["ra", i][:, 128 * g : 128 * (g + 1)],
+                    rhs=a_codes[:, g, cols].bitcast(FP8X4),
+                    rhs_scale=a_scls[:, g, cols],
+                    start=False,
+                    stop=(g == GA - 1),
+                )
+
+        rel_t, ox_t = {}, {}
+
+        def relevance(i, half):
+            if half == 0:
+                rel_t[i] = outs.tile([P, N], F32, name="rel")
+                f_sb[i] = work.tile([P, N], BF16, name="f_sb")
+            cols = slice(512 * half, 512 * (half + 1))
+            nc.vector.tensor_tensor(
+                out=rel_t[i][:, cols], in0=c_acc[half][:], in1=h_sb[i // 2][:, i % 2, cols], op=ALU.mult
+            )
+            nc.vector.tensor_tensor(
+                out=f_sb[i][:, cols].rearrange("p (u w e) -> p u w e", u=2, e=2),
+                in0=c_acc[half][:].rearrange("p (w u e) -> p u w e", u=2, e=2),
+                in1=wt[i][:, cols].rearrange("p (w u e) -> p u w e", u=2, e=2),
+                op=ALU.mult,
+            )
+            if half == 1:
+                nc.sync.dma_start(out=rel_h_v[:, i, :], in_=rel_t[i][:])
+
+        def turn_f(i):
+            grp["f", i] = work.tile([P, N], BF16, name="f_grp", align_bytes=64)
+            transpose_bank(f_sb[i][:].bitcast(F32), 0, 1, grp["f", i][:].bitcast(F32))
+
+        def back(i):
+            ox_t[i] = outs.tile([P, D], F32, name="ox")
+            for c in range(3):
+                acc = b_psum.tile([P, 512], F32, name="x_acc")
+                for g in range(GN):
+                    nc.tensor.matmul_mx(
+                        out=acc[:],
+                        lhsT=codes["f", i][:, 128 * g : 128 * (g + 1)].bitcast(FP8X4),
+                        lhsT_scale=scls["f", i][:, 128 * g : 128 * (g + 1)],
+                        rhs=u_sb[:, g, 1024 * c : 1024 * (c + 1)].bitcast(FP4X4),
+                        rhs_scale=usc[:, D * g + 512 * c : D * g + 512 * (c + 1)],
+                        start=(g == 0),
+                        stop=(g == GN - 1),
+                    )
+                x_acc[c] = acc
+
+        def finish(i):
+            for c in range(3):
+                cols = slice(512 * c, 512 * (c + 1))
+                nc.vector.tensor_tensor(
+                    out=ox_t[i][:, cols], in0=x_acc[c][:], in1=x_sb[i // 2][:, i % 2, cols], op=ALU.mult
+                )
+            nc.sync.dma_start(out=rel_x_v[:, i, :], in_=ox_t[i][:])
+
+        a_codes = keep.tile([P, GA, N], U32, name="a_codes", align_bytes=64)
+        a_scls = keep.tile([P, GA, N], U8, name="a_scls", align_bytes=64)
+        a_grp = {}
+        for g in range(GA):
+            for half in range(2):
+                a_grp[g, half] = keep.tile([P, 512, 4], BF16, name=f"a_grp{g}{half}", align_bytes=64)
+
+        def group_a(engine_copy, g, half):
+            engine_copy(
+                out=a_grp[g, half][:], in_=a_raw[g][:, :, 512 * half : 512 * (half + 1)].rearrange("p j n -> p n j")
+            )
+
+        def quant_a(g, half):
+            cols = slice(512 * half, 512 * (half + 1))
+            nc.vector.quantize_mx(
+                out=a_codes[:, g, cols].bitcast(FP8X4),
+                scales=a_scls[:, g, cols],
+                in_=a_grp[g, half][:].rearrange("p n j -> p (n j)"),
+            )
+
+        widen(0, 0)
+        widen(1, 0)
+        turn_rb(0, 0)
+        turn_ra(0)
+        widen(0, 1)
+        turn_rb(0, 1)
+        widen(1, 1)
+        quant("ra", 0, KA)
+        quant("rb", 0, KB)
+        group_a(nc.vector.tensor_copy, 0, 1)
+        group_a(nc.scalar.copy, 0, 0)
+        group_a(nc.vector.tensor_copy, 1, 1)
+        group_a(nc.scalar.copy, 1, 0)
+        quant_a(0, 1)
+        quant_a(0, 0)
+        quant_a(1, 1)
+        quant_a(1, 0)
+        widen(2, 0)
+        widen(2, 1)
+        reciprocal_d(0)
+        weight_sign(0)
+
+        for s in range(TILES + 1):
+            if s >= 1:
+                turn_f(s - 1)
+            if s + 1 < TILES:
+                turn_ra(s + 1)
+                turn_rb(s + 1, 0)
+                turn_rb(s + 1, 1)
+                reciprocal_d(s + 1)
+            if s + 3 < TILES:
+                widen(s + 3, 0)
+            if s >= 1:
+                quant("f", s - 1, N)
+            if s + 3 < TILES:
+                widen(s + 3, 1)
+            if s + 1 < TILES:
+                quant("ra", s + 1, KA)
+                quant("rb", s + 1, KB)
+                weight_sign(s + 1)
+            if s < TILES:
+                for half in range(2):
+                    product_c(s, half)
+                    relevance(s, half)
+            if s == 0:
+                load_rows("rb", 3)
+                load_rows("ra", 3)
+                load_rows("x", 2)
+            if s == 1:
+                load_rows("d", 3)
+                load_rows("h", 3)
+            if s >= 1:
+                back(s - 1)
+                finish(s - 1)
+            if s == 2:
+                load_rows("x", 3)

@@ -58,12 +58,8 @@ def tile_relevance_step_fanout_s3_kernel(
         nc.gpsimd.memset(bsc[:].bitcast(I32), 0)
         nc.gpsimd.memset(usc[:].bitcast(I32), 0)
 
-        scale_bc = [keep.tile([P, KB // 2], F32, name=f"scale_bc{k}", align_bytes=64) for k in range(2)]
+        rb_scl = keep.tile([P, GB, 4], F32, name="rb_scl")
         a_raw = [araw_pool.tile([P, 4, N], BF16, name="a_raw", align_bytes=64) for g in range(GA)]
-
-        def load_scale(k):
-            half = rb_scale[:, k * KB // 2 : (k + 1) * KB // 2]
-            nc.sync.dma_start(out=scale_bc[k][:], in_=half.rearrange("o k -> (o k)").partition_broadcast(P))
 
         def load_a(g):
             nc.sync.dma_start(out=a_raw[g][:], in_=a[512 * g : 512 * (g + 1), :].rearrange("(p j) n -> p j n", j=4))
@@ -80,10 +76,9 @@ def tile_relevance_step_fanout_s3_kernel(
 
         b_sb = keep.tile([P, GB, 2 * N], U8, name="b_sb", align_bytes=64)
         u_sb = keep.tile([P, GN, 2 * D], U8, name="u_sb", align_bytes=64)
-        load_scale(0)
         load_rows("rb", 0)
-        load_scale(1)
         load_rows("ra", 0)
+        nc.sync.dma_start(out=rb_scl[:], in_=rb_scale[0].rearrange("(g p t) -> p g t", g=GB, t=4))
         load_a(0)
         load_a(1)
         for q in range(4):
@@ -109,18 +104,16 @@ def tile_relevance_step_fanout_s3_kernel(
             load_rows(name, 2)
         load_rows("x", 1)
 
-        rbw, grp, codes, scls, sgn_h, wt, f_sb, f_codes, f_scls = {}, {}, {}, {}, {}, {}, {}, {}, {}
+        rb_xt, rbw, grp, codes, scls, sgn_h, wt, f_sb, f_codes, f_scls = {}, {}, {}, {}, {}, {}, {}, {}, {}, {}
         c_acc, x_acc, recip = {}, {}, {}
 
         def widen(i, part):
             if part == 0:
                 rbw[i] = wide.tile([P, KB], BF16, name="rbw", align_bytes=64)
             cols = slice(part * KB // 2, (part + 1) * KB // 2)
-            nc.vector.tensor_tensor(
-                out=rbw[i][:, cols], in0=rb_sb[i // 2][:, i % 2, cols].bitcast(FP8), in1=scale_bc[part][:], op=ALU.mult
-            )
+            nc.scalar.copy(out=rbw[i][:, cols], in_=rb_sb[i // 2][:, i % 2, cols].bitcast(FP8))
 
-        def transpose_bank(words, base, step, out_words):
+        def transpose_bank(words, base, step):
             xt = t_psum.tile([P, 2, 2, P], F32, name="xt")
             for g in range(2):
                 for u in range(2):
@@ -131,20 +124,32 @@ def tile_relevance_step_fanout_s3_kernel(
                         first = base + 256 * g + 128 * u
                         src = words[:, first : first + 128]
                     nc.tensor.transpose(xt[:, g, u, :], src, ident[:])
+            return xt
+
+        def interleave(xt, out_words):
             nc.scalar.copy(
                 out=out_words.rearrange("p (g r u) -> p g r u", g=2, u=2), in_=xt[:].rearrange("p g u r -> p g r u")
             )
 
         def turn_ra(i):
             grp["ra", i] = work.tile([P, KA], BF16, name="ra_grp", align_bytes=64)
-            transpose_bank(ra_sb[i // 2][:, i % 2, :].bitcast(F32), 0, 2, grp["ra", i][:].bitcast(F32))
+            interleave(transpose_bank(ra_sb[i // 2][:, i % 2, :].bitcast(F32), 0, 2), grp["ra", i][:].bitcast(F32))
 
         def turn_rb(i, half):
             if half == 0:
                 grp["rb", i] = work.tile([P, KB], BF16, name="rb_grp", align_bytes=64)
-            transpose_bank(
-                rbw[i][:].bitcast(F32), 512 * half, 2, grp["rb", i][:, 1024 * half : 1024 * (half + 1)].bitcast(F32)
-            )
+            rb_xt[half] = transpose_bank(rbw[i][:].bitcast(F32), 512 * half, 2)
+
+        def scale_rb(i, half):
+            for k in range(2):
+                g = 2 * half + k
+                bank = rb_xt[half][:].rearrange("p g u r -> p (g u r)").bitcast(BF16)
+                nc.vector.tensor_tensor(
+                    out=grp["rb", i][:, 512 * g : 512 * (g + 1)].rearrange("p (r u e) -> p r u e", u=2, e=2),
+                    in0=bank[:, 512 * k : 512 * (k + 1)].rearrange("p (u r e) -> p r u e", u=2, e=2),
+                    in1=rb_scl[:, g, :].rearrange("p (o u e) -> p o u e", o=1, u=2).to_broadcast([P, P, 2, 2]),
+                    op=ALU.mult,
+                )
 
         def quant(kind, i, width):
             codes[kind, i] = work.tile([P, width // 4], U32, name=f"{kind}_codes", align_bytes=64)
@@ -172,13 +177,11 @@ def tile_relevance_step_fanout_s3_kernel(
             wt[i] = work.tile([P, N], F32, name="wt")
             nc.gpsimd.tensor_tensor(out=wt[i][:], in0=sh[:], in1=recip[i][:], op=ALU.mult)
 
-        def product_c(i, half):
-            acc = c_psum.tile([P, 512], F32, name="c_acc")
-            c_acc[half] = acc
-            cols = slice(512 * half, 512 * (half + 1))
+        def product_b(i, half):
+            c_acc[half] = c_psum.tile([P, 512], F32, name="c_acc")
             for g in range(GB):
                 nc.tensor.matmul_mx(
-                    out=acc[:],
+                    out=c_acc[half][:],
                     lhsT=codes["rb", i][:, 128 * g : 128 * (g + 1)].bitcast(FP8X4),
                     lhsT_scale=scls["rb", i][:, 128 * g : 128 * (g + 1)],
                     rhs=b_sb[:, g, 1024 * half : 1024 * (half + 1)].bitcast(FP4X4),
@@ -186,9 +189,12 @@ def tile_relevance_step_fanout_s3_kernel(
                     start=(g == 0),
                     stop=False,
                 )
+
+        def product_a(i, half):
+            cols = slice(512 * half, 512 * (half + 1))
             for g in range(GA):
                 nc.tensor.matmul_mx(
-                    out=acc[:],
+                    out=c_acc[half][:],
                     lhsT=codes["ra", i][:, 128 * g : 128 * (g + 1)].bitcast(FP8X4),
                     lhsT_scale=scls["ra", i][:, 128 * g : 128 * (g + 1)],
                     rhs=a_codes[:, g, cols].bitcast(FP8X4),
@@ -218,7 +224,7 @@ def tile_relevance_step_fanout_s3_kernel(
 
         def turn_f(i):
             grp["f", i] = work.tile([P, N], BF16, name="f_grp", align_bytes=64)
-            transpose_bank(f_sb[i][:].bitcast(F32), 0, 1, grp["f", i][:].bitcast(F32))
+            interleave(transpose_bank(f_sb[i][:].bitcast(F32), 0, 1), grp["f", i][:].bitcast(F32))
 
         def back(i):
             ox_t[i] = outs.tile([P, D], F32, name="ox")
@@ -265,24 +271,24 @@ def tile_relevance_step_fanout_s3_kernel(
             )
 
         widen(0, 0)
-        widen(1, 0)
         turn_rb(0, 0)
-        turn_ra(0)
+        scale_rb(0, 0)
         widen(0, 1)
         turn_rb(0, 1)
-        widen(1, 1)
-        quant("ra", 0, KA)
-        quant("rb", 0, KB)
+        scale_rb(0, 1)
+        turn_ra(0)
         group_a(nc.vector.tensor_copy, 0, 1)
+        quant("rb", 0, KB)
+        quant("ra", 0, KA)
         group_a(nc.scalar.copy, 0, 0)
+        widen(1, 0)
+        widen(1, 1)
         group_a(nc.vector.tensor_copy, 1, 1)
-        group_a(nc.scalar.copy, 1, 0)
         quant_a(0, 1)
         quant_a(0, 0)
+        group_a(nc.scalar.copy, 1, 0)
         quant_a(1, 1)
         quant_a(1, 0)
-        widen(2, 0)
-        widen(2, 1)
         reciprocal_d(0)
         weight_sign(0)
 
@@ -292,21 +298,27 @@ def tile_relevance_step_fanout_s3_kernel(
             if s + 1 < TILES:
                 turn_ra(s + 1)
                 turn_rb(s + 1, 0)
+                scale_rb(s + 1, 0)
                 turn_rb(s + 1, 1)
-                reciprocal_d(s + 1)
-            if s + 3 < TILES:
-                widen(s + 3, 0)
+            if s + 2 < TILES:
+                widen(s + 2, 0)
+                widen(s + 2, 1)
             if s >= 1:
                 quant("f", s - 1, N)
-            if s + 3 < TILES:
-                widen(s + 3, 1)
             if s + 1 < TILES:
+                reciprocal_d(s + 1)
+                scale_rb(s + 1, 1)
                 quant("ra", s + 1, KA)
                 quant("rb", s + 1, KB)
                 weight_sign(s + 1)
             if s < TILES:
+                if s == 0:
+                    product_b(s, 0)
+                    product_b(s, 1)
                 for half in range(2):
-                    product_c(s, half)
+                    if s > 0:
+                        product_b(s, half)
+                    product_a(s, half)
                     relevance(s, half)
             if s == 0:
                 load_rows("rb", 3)

@@ -19,6 +19,7 @@ ACT = mybir.ActivationFunctionType
 
 P = 128
 TILES = M // P
+COLS = 512
 GA, GB, GN = KA // 512, KB // 512, N // 512
 SIGN_BITS = -2147450880
 
@@ -29,11 +30,13 @@ def tile_relevance_step_fanout_s3_kernel(
     nc = tc.nc
     with ExitStack() as ctx:
         keep = ctx.enter_context(tc.tile_pool(name="keep", bufs=1))
-        stream = ctx.enter_context(tc.tile_pool(name="stream", bufs=3))
-        araw_pool = ctx.enter_context(tc.tile_pool(name="araw", bufs=2))
+        stream = ctx.enter_context(tc.tile_pool(name="stream", bufs=4))
+        xin = ctx.enter_context(tc.tile_pool(name="xin", bufs=3))
+        araw_pool = ctx.enter_context(tc.tile_pool(name="araw", bufs=4))
+        agrp_pool = ctx.enter_context(tc.tile_pool(name="agrp", bufs=2))
         work = ctx.enter_context(tc.tile_pool(name="work", bufs=2))
-        wide = ctx.enter_context(tc.tile_pool(name="wide", bufs=4))
-        outs = ctx.enter_context(tc.tile_pool(name="outs", bufs=2))
+        deep = ctx.enter_context(tc.tile_pool(name="deep", bufs=3))
+        outs = ctx.enter_context(tc.tile_pool(name="outs", bufs=3))
         c_psum = ctx.enter_context(tc.psum_pool(name="c_psum", bufs=2))
         b_psum = ctx.enter_context(tc.psum_pool(name="b_psum", bufs=3))
         t_psum = ctx.enter_context(tc.psum_pool(name="t_psum", bufs=3))
@@ -42,78 +45,83 @@ def tile_relevance_step_fanout_s3_kernel(
         def row_view(t):
             return t.rearrange("(p i) k -> p i k", i=TILES)
 
-        ra_v, rb_v, h_v, d_v, x_v = [row_view(t) for t in (ra, rb_bytes, h, d, x)]
+        views = {"ra": row_view(ra), "rb": row_view(rb_bytes), "h": row_view(h), "d": row_view(d), "x": row_view(x)}
         rel_h_v, rel_x_v = row_view(rel_h), row_view(rel_x)
-        ra_sb, rb_sb, h_sb, d_sb, x_sb = {}, {}, {}, {}, {}
+        rows = {}
 
-        def load_pair(store, name, view, width, dtype, j):
-            t = stream.tile([P, 2, width], dtype, name=name, align_bytes=64)
-            nc.sync.dma_start(out=t[:], in_=view[:, 2 * j : 2 * j + 2, :])
-            store[j] = t
+        def load_rows(name, first, count):
+            view = views[name]
+            pool = xin if name == "x" else stream
+            t = pool.tile([P, count, view.shape[2]], view.dtype, name=name + "_in", align_bytes=64)
+            nc.sync.dma_start(out=t[:], in_=view[:, first : first + count, :])
+            for k in range(count):
+                rows[name, first + k] = t[:, k, :]
 
         ident = keep.tile([P, P], F32, name="ident")
         make_identity(nc, ident[:])
         bsc = keep.tile([P, GB * N], U8, name="bsc", align_bytes=64)
         usc = keep.tile([P, GN * D], U8, name="usc", align_bytes=64)
-        nc.gpsimd.memset(bsc[:].bitcast(I32), 0)
-        nc.gpsimd.memset(usc[:].bitcast(I32), 0)
-
+        nc.vector.memset(bsc[:].bitcast(I32), 0)
+        nc.vector.memset(usc[:].bitcast(I32), 0)
         rb_scl = keep.tile([P, GB, 4], F32, name="rb_scl")
-        a_raw = [araw_pool.tile([P, 4, N], BF16, name="a_raw", align_bytes=64) for g in range(GA)]
-
-        def load_a(g):
-            nc.sync.dma_start(out=a_raw[g][:], in_=a[512 * g : 512 * (g + 1), :].rearrange("(p j) n -> p j n", j=4))
-
-        def load_rows(name, j):
-            store, view, width, dtype = {
-                "ra": (ra_sb, ra_v, KA, BF16),
-                "rb": (rb_sb, rb_v, KB, U8),
-                "h": (h_sb, h_v, N, BF16),
-                "d": (d_sb, d_v, N, BF16),
-                "x": (x_sb, x_v, D, BF16),
-            }[name]
-            load_pair(store, name + "_in", view, width, dtype, j)
-
-        b_sb = keep.tile([P, GB, 2 * N], U8, name="b_sb", align_bytes=64)
+        b_sb = [keep.tile([P, GB, 2 * COLS], U8, name=f"b_sb{k}", align_bytes=64) for k in range(2)]
         u_sb = keep.tile([P, GN, 2 * D], U8, name="u_sb", align_bytes=64)
-        load_rows("rb", 0)
-        load_rows("ra", 0)
+        a_raw = {}
+
+        def load_a(g, half):
+            a_raw[g, half] = araw_pool.tile([P, 4, COLS], BF16, name="a_raw", align_bytes=64)
+            src = a[512 * g : 512 * (g + 1), COLS * half : COLS * (half + 1)]
+            nc.sync.dma_start(out=a_raw[g, half][:], in_=src.rearrange("(p j) n -> p j n", j=4))
+
+        def load_b(half):
+            cols = slice(2 * COLS * half, 2 * COLS * (half + 1))
+            nc.sync.dma_start(out=b_sb[half][:], in_=b_words[:, :, cols].rearrange("g p c -> p g c"))
+
+        def load_scales(tile, src, groups):
+            for q in range(4):
+                nc.sync.dma_start(
+                    out=tile[32 * q : 32 * q + 4, :].bitcast(I32).rearrange("p (g n) -> p g n", g=groups),
+                    in_=src[:, 4 * q : 4 * q + 4, :].bitcast(I32).rearrange("g q n -> q g n"),
+                )
+
+        load_rows("rb", 0, 1)
         nc.sync.dma_start(out=rb_scl[:], in_=rb_scale[0].rearrange("(g p t) -> p g t", g=GB, t=4))
-        load_a(0)
-        load_a(1)
-        for q in range(4):
-            nc.sync.dma_start(
-                out=bsc[32 * q : 32 * q + 4, :].bitcast(I32).rearrange("p (g n) -> p g n", g=GB),
-                in_=b_scales[:, 4 * q : 4 * q + 4, :].bitcast(I32).rearrange("g q n -> q g n"),
-            )
-        for q in range(4):
-            nc.sync.dma_start(
-                out=usc[32 * q : 32 * q + 4, :].bitcast(I32).rearrange("p (g n) -> p g n", g=GN),
-                in_=u_scales[:, 4 * q : 4 * q + 4, :].bitcast(I32).rearrange("g q n -> q g n"),
-            )
-        nc.sync.dma_start(out=b_sb[:], in_=b_words.rearrange("g p c -> p g c"))
-        load_rows("rb", 1)
-        load_rows("d", 0)
-        load_rows("h", 0)
-        load_rows("ra", 1)
+        load_scales(bsc, b_scales, GB)
+        load_a(1, 0)
+        load_a(0, 0)
+        load_b(0)
+        load_rows("ra", 0, 1)
+        load_a(0, 1)
+        load_a(1, 1)
+        load_rows("rb", 1, 1)
+        load_b(1)
+        load_rows("d", 0, 1)
+        load_rows("h", 0, 1)
+        load_rows("ra", 1, 1)
+        load_rows("rb", 2, 2)
+        load_rows("ra", 2, 2)
+        load_rows("d", 1, 1)
+        load_rows("h", 1, 1)
+        load_rows("rb", 4, 2)
+        load_rows("ra", 4, 2)
+        load_rows("d", 2, 2)
+        load_rows("h", 2, 2)
+        load_scales(usc, u_scales, GN)
         nc.sync.dma_start(out=u_sb[:], in_=u_words.rearrange("g p c -> p g c"))
-        for name in ("d", "h"):
-            load_rows(name, 1)
-        load_rows("x", 0)
-        for name in ("rb", "ra", "d", "h"):
-            load_rows(name, 2)
-        load_rows("x", 1)
+        load_rows("x", 0, 2)
+        load_rows("d", 4, 2)
+        load_rows("h", 4, 2)
 
-        rb_xt, rbw, grp, codes, scls, sgn_h, wt, f_sb, f_codes, f_scls = {}, {}, {}, {}, {}, {}, {}, {}, {}, {}
-        c_acc, x_acc, recip = {}, {}, {}
+        rbw, banks, grp, codes, scls, recip, sgn, f_sb = {}, {}, {}, {}, {}, {}, {}, {}
+        c_acc, x_acc, rel_t, ox_t = {}, {}, {}, {}
 
-        def widen(i, part):
-            if part == 0:
-                rbw[i] = wide.tile([P, KB], BF16, name="rbw", align_bytes=64)
-            cols = slice(part * KB // 2, (part + 1) * KB // 2)
-            nc.scalar.copy(out=rbw[i][:, cols], in_=rb_sb[i // 2][:, i % 2, cols].bitcast(FP8))
+        def widen(i, engine_copy):
+            rbw[i] = deep.tile([P, KB], BF16, name="rbw", align_bytes=64)
+            for k in range(1):
+                cols = slice(k * KB // 1, (k + 1) * KB // 1)
+                engine_copy(out=rbw[i][:, cols], in_=rows["rb", i][:, cols].bitcast(FP8))
 
-        def transpose_bank(words, base, step):
+        def turn(words, base, step):
             xt = t_psum.tile([P, 2, 2, P], F32, name="xt")
             for g in range(2):
                 for u in range(2):
@@ -126,24 +134,29 @@ def tile_relevance_step_fanout_s3_kernel(
                     nc.tensor.transpose(xt[:, g, u, :], src, ident[:])
             return xt
 
-        def interleave(xt, out_words):
+        def turn_and_group(kind, i, words, step):
+            xt = turn(words, 0, step)
+            grp[kind, i] = work.tile([P, 1024], BF16, name=kind + "_grp", align_bytes=64)
             nc.scalar.copy(
-                out=out_words.rearrange("p (g r u) -> p g r u", g=2, u=2), in_=xt[:].rearrange("p g u r -> p g r u")
+                out=grp[kind, i][:].bitcast(F32).rearrange("p (g r u) -> p g r u", g=2, u=2),
+                in_=xt[:].rearrange("p g u r -> p g r u"),
             )
 
         def turn_ra(i):
-            grp["ra", i] = work.tile([P, KA], BF16, name="ra_grp", align_bytes=64)
-            interleave(transpose_bank(ra_sb[i // 2][:, i % 2, :].bitcast(F32), 0, 2), grp["ra", i][:].bitcast(F32))
+            turn_and_group("ra", i, rows["ra", i].bitcast(F32), 2)
+
+        def turn_f(i):
+            turn_and_group("f", i, f_sb[i][:].bitcast(F32), 1)
 
         def turn_rb(i, half):
-            if half == 0:
-                grp["rb", i] = work.tile([P, KB], BF16, name="rb_grp", align_bytes=64)
-            rb_xt[half] = transpose_bank(rbw[i][:].bitcast(F32), 512 * half, 2)
+            banks[half] = turn(rbw[i][:].bitcast(F32), 512 * half, 2)
 
         def scale_rb(i, half):
+            if half == 0:
+                grp["rb", i] = work.tile([P, KB], BF16, name="rb_grp", align_bytes=64)
+            bank = banks[half][:].rearrange("p g u r -> p (g u r)").bitcast(BF16)
             for k in range(2):
                 g = 2 * half + k
-                bank = rb_xt[half][:].rearrange("p g u r -> p (g u r)").bitcast(BF16)
                 nc.vector.tensor_tensor(
                     out=grp["rb", i][:, 512 * g : 512 * (g + 1)].rearrange("p (r u e) -> p r u e", u=2, e=2),
                     in0=bank[:, 512 * k : 512 * (k + 1)].rearrange("p (u r e) -> p r u e", u=2, e=2),
@@ -151,184 +164,187 @@ def tile_relevance_step_fanout_s3_kernel(
                     op=ALU.mult,
                 )
 
-        def quant(kind, i, width):
-            codes[kind, i] = work.tile([P, width // 4], U32, name=f"{kind}_codes", align_bytes=64)
-            scls[kind, i] = work.tile([P, width // 4], U8, name=f"{kind}_scls", align_bytes=64)
+        def quant(kind, i):
+            width = grp[kind, i].shape[1]
+            codes[kind, i] = deep.tile([P, width // 4], U32, name=kind + "_codes", align_bytes=64)
+            scls[kind, i] = deep.tile([P, width // 4], U8, name=kind + "_scls", align_bytes=64)
             nc.vector.quantize_mx(out=codes[kind, i][:].bitcast(FP8X4), scales=scls[kind, i][:], in_=grp[kind, i][:])
 
         def reciprocal_d(i):
-            dt = d_sb[i // 2][:, i % 2, :]
             y = work.tile([P, N], F32, name="y")
-            nc.scalar.activation(out=y[:], in_=dt, func=ACT.Abs_reciprocal_sqrt)
+            nc.scalar.activation(out=y[:], in_=rows["d", i], func=ACT.Abs_reciprocal_sqrt)
             nc.scalar.activation(out=y[:], in_=y[:], func=ACT.Square)
             recip[i] = y
+            sgn[i] = work.tile([P, N], BF16, name="sgn")
+            for half in range(2):
+                cols = slice(COLS * half, COLS * (half + 1))
+                nc.scalar.activation(
+                    out=sgn[i][:, cols].rearrange("p (u w e) -> p u w e", u=2, e=2),
+                    in_=rows["d", i][:, cols].rearrange("p (w u e) -> p u w e", u=2, e=2),
+                    func=ACT.Sign,
+                )
 
-        def weight_sign(i):
-            dt, ht = d_sb[i // 2][:, i % 2, :], h_sb[i // 2][:, i % 2, :]
-            sh = work.tile([P, N], BF16, name="sh")
-            nc.vector.scalar_tensor_tensor(
-                out=sh[:].bitcast(I32),
-                in0=dt.bitcast(I32),
-                scalar=SIGN_BITS,
-                in1=ht.bitcast(I32),
-                op0=ALU.bitwise_and,
-                op1=ALU.bitwise_xor,
+        def signed(i, half):
+            cols = slice(COLS * half, COLS * (half + 1))
+            nc.vector.tensor_tensor(out=f_sb[i][:, cols], in0=f_sb[i][:, cols], in1=sgn[i][:, cols], op=ALU.mult)
+
+        def mx(out, kind, i, g, moving, moving_scale, start, stop):
+            cols = slice(128 * g, 128 * (g + 1))
+            nc.tensor.matmul_mx(
+                out=out,
+                lhsT=codes[kind, i][:, cols].bitcast(FP8X4),
+                lhsT_scale=scls[kind, i][:, cols],
+                rhs=moving,
+                rhs_scale=moving_scale,
+                start=start,
+                stop=stop,
             )
-            wt[i] = work.tile([P, N], F32, name="wt")
-            nc.gpsimd.tensor_tensor(out=wt[i][:], in0=sh[:], in1=recip[i][:], op=ALU.mult)
 
-        def product_b(i, half):
-            c_acc[half] = c_psum.tile([P, 512], F32, name="c_acc")
+        def product_c(i, half):
+            acc = c_psum.tile([P, COLS], F32, name="c_acc")
+            c_acc[half] = acc
             for g in range(GB):
-                nc.tensor.matmul_mx(
-                    out=c_acc[half][:],
-                    lhsT=codes["rb", i][:, 128 * g : 128 * (g + 1)].bitcast(FP8X4),
-                    lhsT_scale=scls["rb", i][:, 128 * g : 128 * (g + 1)],
-                    rhs=b_sb[:, g, 1024 * half : 1024 * (half + 1)].bitcast(FP4X4),
-                    rhs_scale=bsc[:, N * g + 512 * half : N * g + 512 * (half + 1)],
-                    start=(g == 0),
-                    stop=False,
-                )
-
-        def product_a(i, half):
-            cols = slice(512 * half, 512 * (half + 1))
+                moving = b_sb[half][:, g, :].bitcast(FP4X4)
+                scale = bsc[:, N * g + COLS * half : N * g + COLS * (half + 1)]
+                mx(acc[:], "rb", i, g, moving, scale, g == 0, False)
             for g in range(GA):
-                nc.tensor.matmul_mx(
-                    out=c_acc[half][:],
-                    lhsT=codes["ra", i][:, 128 * g : 128 * (g + 1)].bitcast(FP8X4),
-                    lhsT_scale=scls["ra", i][:, 128 * g : 128 * (g + 1)],
-                    rhs=a_codes[:, g, cols].bitcast(FP8X4),
-                    rhs_scale=a_scls[:, g, cols],
-                    start=False,
-                    stop=(g == GA - 1),
-                )
+                mx(acc[:], "ra", i, g, a_codes[g, half][:].bitcast(FP8X4), a_scls[g, half][:], False, g == GA - 1)
 
-        rel_t, ox_t = {}, {}
-
-        def relevance(i, half):
+        def relevance(i, half, engine):
             if half == 0:
                 rel_t[i] = outs.tile([P, N], F32, name="rel")
                 f_sb[i] = work.tile([P, N], BF16, name="f_sb")
-            cols = slice(512 * half, 512 * (half + 1))
-            nc.vector.tensor_tensor(
-                out=rel_t[i][:, cols], in0=c_acc[half][:], in1=h_sb[i // 2][:, i % 2, cols], op=ALU.mult
-            )
-            nc.vector.tensor_tensor(
+            cols = slice(COLS * half, COLS * (half + 1))
+            nc.vector.tensor_tensor(out=rel_t[i][:, cols], in0=c_acc[half][:], in1=rows["h", i][:, cols], op=ALU.mult)
+            engine.tensor_tensor(
                 out=f_sb[i][:, cols].rearrange("p (u w e) -> p u w e", u=2, e=2),
-                in0=c_acc[half][:].rearrange("p (w u e) -> p u w e", u=2, e=2),
-                in1=wt[i][:, cols].rearrange("p (w u e) -> p u w e", u=2, e=2),
+                in0=rel_t[i][:, cols].rearrange("p (w u e) -> p u w e", u=2, e=2),
+                in1=recip[i][:, cols].rearrange("p (w u e) -> p u w e", u=2, e=2),
                 op=ALU.mult,
             )
             if half == 1:
                 nc.sync.dma_start(out=rel_h_v[:, i, :], in_=rel_t[i][:])
 
-        def turn_f(i):
-            grp["f", i] = work.tile([P, N], BF16, name="f_grp", align_bytes=64)
-            interleave(transpose_bank(f_sb[i][:].bitcast(F32), 0, 1), grp["f", i][:].bitcast(F32))
-
         def back(i):
-            ox_t[i] = outs.tile([P, D], F32, name="ox")
             for c in range(3):
-                acc = b_psum.tile([P, 512], F32, name="x_acc")
+                acc = b_psum.tile([P, COLS], F32, name="x_acc")
                 for g in range(GN):
-                    nc.tensor.matmul_mx(
-                        out=acc[:],
-                        lhsT=codes["f", i][:, 128 * g : 128 * (g + 1)].bitcast(FP8X4),
-                        lhsT_scale=scls["f", i][:, 128 * g : 128 * (g + 1)],
-                        rhs=u_sb[:, g, 1024 * c : 1024 * (c + 1)].bitcast(FP4X4),
-                        rhs_scale=usc[:, D * g + 512 * c : D * g + 512 * (c + 1)],
-                        start=(g == 0),
-                        stop=(g == GN - 1),
-                    )
-                x_acc[c] = acc
+                    moving = u_sb[:, g, 2 * COLS * c : 2 * COLS * (c + 1)].bitcast(FP4X4)
+                    scale = usc[:, D * g + COLS * c : D * g + COLS * (c + 1)]
+                    mx(acc[:], "f", i, g, moving, scale, g == 0, g == GN - 1)
+                x_acc[i, c] = acc
 
         def finish(i):
+            ox_t[i] = outs.tile([P, D], F32, name="ox")
             for c in range(3):
-                cols = slice(512 * c, 512 * (c + 1))
-                nc.vector.tensor_tensor(
-                    out=ox_t[i][:, cols], in0=x_acc[c][:], in1=x_sb[i // 2][:, i % 2, cols], op=ALU.mult
-                )
-            nc.sync.dma_start(out=rel_x_v[:, i, :], in_=ox_t[i][:])
+                cols = slice(COLS * c, COLS * (c + 1))
+                nc.vector.tensor_tensor(out=ox_t[i][:, cols], in0=x_acc[i, c][:], in1=rows["x", i][:, cols], op=ALU.mult)
+                if i == TILES - 1:
+                    nc.sync.dma_start(out=rel_x_v[:, i, cols], in_=ox_t[i][:, cols])
+            if i < TILES - 1:
+                nc.sync.dma_start(out=rel_x_v[:, i, :], in_=ox_t[i][:])
 
-        a_codes = keep.tile([P, GA, N], U32, name="a_codes", align_bytes=64)
-        a_scls = keep.tile([P, GA, N], U8, name="a_scls", align_bytes=64)
-        a_grp = {}
-        for g in range(GA):
-            for half in range(2):
-                a_grp[g, half] = keep.tile([P, 512, 4], BF16, name=f"a_grp{g}{half}", align_bytes=64)
+        a_grp, a_codes, a_scls = {}, {}, {}
+
+        def gpsimd_copy(out, in_):
+            nc.gpsimd.tensor_scalar(out=out, in0=in_, scalar1=1.0, scalar2=0.0, op0=ALU.mult, op1=ALU.add)
 
         def group_a(engine_copy, g, half):
-            engine_copy(
-                out=a_grp[g, half][:], in_=a_raw[g][:, :, 512 * half : 512 * (half + 1)].rearrange("p j n -> p n j")
-            )
+            a_grp[g, half] = agrp_pool.tile([P, COLS, 4], BF16, name="a_grp", align_bytes=64)
+            engine_copy(out=a_grp[g, half][:], in_=a_raw[g, half][:].rearrange("p j n -> p n j"))
 
         def quant_a(g, half):
-            cols = slice(512 * half, 512 * (half + 1))
+            a_codes[g, half] = keep.tile([P, COLS], U32, name=f"a_codes{g}{half}", align_bytes=64)
+            a_scls[g, half] = keep.tile([P, COLS], U8, name=f"a_scls{g}{half}", align_bytes=64)
             nc.vector.quantize_mx(
-                out=a_codes[:, g, cols].bitcast(FP8X4),
-                scales=a_scls[:, g, cols],
+                out=a_codes[g, half][:].bitcast(FP8X4),
+                scales=a_scls[g, half][:],
                 in_=a_grp[g, half][:].rearrange("p n j -> p (n j)"),
             )
 
-        widen(0, 0)
+        widen(0, nc.vector.tensor_copy)
         turn_rb(0, 0)
-        scale_rb(0, 0)
-        widen(0, 1)
         turn_rb(0, 1)
+        group_a(nc.scalar.copy, 0, 0)
+        scale_rb(0, 0)
+        group_a(gpsimd_copy, 1, 0)
         scale_rb(0, 1)
         turn_ra(0)
-        group_a(nc.vector.tensor_copy, 0, 1)
-        quant("rb", 0, KB)
-        quant("ra", 0, KA)
-        group_a(nc.scalar.copy, 0, 0)
-        widen(1, 0)
-        widen(1, 1)
-        group_a(nc.vector.tensor_copy, 1, 1)
-        quant_a(0, 1)
+        quant("rb", 0)
         quant_a(0, 0)
-        group_a(nc.scalar.copy, 1, 0)
-        quant_a(1, 1)
+        quant("ra", 0)
         quant_a(1, 0)
+        product_c(0, 0)
+        group_a(nc.scalar.copy, 0, 1)
+        group_a(nc.vector.tensor_copy, 1, 1)
+        widen(1, nc.vector.tensor_copy)
+        turn_rb(1, 0)
+        turn_rb(1, 1)
+        turn_ra(1)
+        quant_a(0, 1)
+        quant_a(1, 1)
         reciprocal_d(0)
-        weight_sign(0)
+        relevance(0, 0, nc.gpsimd)
+        scale_rb(1, 0)
+        scale_rb(1, 1)
+        quant("ra", 1)
+        product_c(0, 1)
+        quant("rb", 1)
+        widen(2, nc.vector.tensor_copy)
+        relevance(0, 1, nc.gpsimd)
+        turn_ra(2)
+        turn_rb(2, 0)
+        scale_rb(2, 0)
+        turn_rb(2, 1)
+        scale_rb(2, 1)
+        quant("ra", 2)
+        quant("rb", 2)
+        reciprocal_d(1)
+        signed(0, 0)
+        signed(0, 1)
+        widen(3, nc.scalar.copy)
+        load_rows("rb", 6, 2)
+        load_rows("ra", 6, 2)
 
-        for s in range(TILES + 1):
-            if s >= 1:
-                turn_f(s - 1)
-            if s + 1 < TILES:
-                turn_ra(s + 1)
-                turn_rb(s + 1, 0)
-                scale_rb(s + 1, 0)
-                turn_rb(s + 1, 1)
+        for s in range(1, TILES):
+            last = s == TILES - 1
+            product_c(s, 0)
+            relevance(s, 0, nc.vector if last else nc.gpsimd)
+            if s >= 2 and not last:
+                finish(s - 2)
+            turn_f(s - 1)
             if s + 2 < TILES:
-                widen(s + 2, 0)
-                widen(s + 2, 1)
-            if s >= 1:
-                quant("f", s - 1, N)
+                turn_ra(s + 2)
+            quant("f", s - 1)
+            if last:
+                finish(s - 2)
+            if s + 2 < TILES:
+                quant("ra", s + 2)
+            product_c(s, 1)
+            relevance(s, 1, nc.vector if last else nc.gpsimd)
+            if s + 3 < TILES:
+                widen(s + 3, nc.scalar.copy)
             if s + 1 < TILES:
                 reciprocal_d(s + 1)
-                scale_rb(s + 1, 1)
-                quant("ra", s + 1, KA)
-                quant("rb", s + 1, KB)
-                weight_sign(s + 1)
-            if s < TILES:
-                if s == 0:
-                    product_b(s, 0)
-                    product_b(s, 1)
-                for half in range(2):
-                    if s > 0:
-                        product_b(s, half)
-                    product_a(s, half)
-                    relevance(s, half)
-            if s == 0:
-                load_rows("rb", 3)
-                load_rows("ra", 3)
-                load_rows("x", 2)
+            if s + 2 < TILES:
+                turn_rb(s + 2, 0)
+                scale_rb(s + 2, 0)
+                turn_rb(s + 2, 1)
+                scale_rb(s + 2, 1)
+                quant("rb", s + 2)
+            signed(s, 0)
+            signed(s, 1)
+            back(s - 1)
             if s == 1:
-                load_rows("d", 3)
-                load_rows("h", 3)
-            if s >= 1:
-                back(s - 1)
-                finish(s - 1)
+                load_rows("x", 2, 2)
+                load_rows("d", 6, 2)
+                load_rows("h", 6, 2)
             if s == 2:
-                load_rows("x", 3)
+                load_rows("x", 4, 2)
+            if s == 4:
+                load_rows("x", 6, 2)
+        turn_f(TILES - 1)
+        finish(TILES - 2)
+        quant("f", TILES - 1)
+        back(TILES - 1)
+        finish(TILES - 1)

@@ -11,17 +11,19 @@ BF16 = mybir.dt.bfloat16
 I32 = mybir.dt.int32
 U32 = mybir.dt.uint32
 U8 = mybir.dt.uint8
-FP8 = mybir.dt.float8_e4m3fn
-FP8X4 = mybir.dt.float8_e4m3fn_x4
-FP4X4 = mybir.dt.float4_e2m1fn_x4
+E4M3 = mybir.dt.float8_e4m3fn
+E4M3X4 = mybir.dt.float8_e4m3fn_x4
+E2M1X4 = mybir.dt.float4_e2m1fn_x4
 ALU = mybir.AluOpType
 ACT = mybir.ActivationFunctionType
 
 P = 128
 TILES = M // P
+PASS = 512
 COLS = 512
-GA, GB, GN = KA // 512, KB // 512, N // 512
-SIGN_BITS = -2147450880
+GA, GB, GN = KA // PASS, KB // PASS, N // PASS
+X_CHUNKS = D // COLS
+LAST = TILES - 1
 
 
 def tile_relevance_step_fanout_s3_kernel(
@@ -31,310 +33,369 @@ def tile_relevance_step_fanout_s3_kernel(
     with ExitStack() as ctx:
         keep = ctx.enter_context(tc.tile_pool(name="keep", bufs=1))
         stream = ctx.enter_context(tc.tile_pool(name="stream", bufs=4))
-        xin = ctx.enter_context(tc.tile_pool(name="xin", bufs=3))
-        araw_pool = ctx.enter_context(tc.tile_pool(name="araw", bufs=4))
-        agrp_pool = ctx.enter_context(tc.tile_pool(name="agrp", bufs=2))
+        stream_x = ctx.enter_context(tc.tile_pool(name="stream_x", bufs=3))
+        a_raw_pool = ctx.enter_context(tc.tile_pool(name="a_raw", bufs=4))
+        a_grouped_pool = ctx.enter_context(tc.tile_pool(name="a_grouped", bufs=2))
         work = ctx.enter_context(tc.tile_pool(name="work", bufs=2))
-        deep = ctx.enter_context(tc.tile_pool(name="deep", bufs=3))
-        outs = ctx.enter_context(tc.tile_pool(name="outs", bufs=3))
+        ahead = ctx.enter_context(tc.tile_pool(name="ahead", bufs=3))
+        results = ctx.enter_context(tc.tile_pool(name="results", bufs=3))
         c_psum = ctx.enter_context(tc.psum_pool(name="c_psum", bufs=2))
-        b_psum = ctx.enter_context(tc.psum_pool(name="b_psum", bufs=3))
-        t_psum = ctx.enter_context(tc.psum_pool(name="t_psum", bufs=3))
+        x_psum = ctx.enter_context(tc.psum_pool(name="x_psum", bufs=3))
+        turn_psum = ctx.enter_context(tc.psum_pool(name="turn_psum", bufs=3))
         ctx.enter_context(tc.manual_schedule())
 
-        def row_view(t):
-            return t.rearrange("(p i) k -> p i k", i=TILES)
+        def by_row_tile(tensor):
+            return tensor.rearrange("(p i) k -> p i k", i=TILES)
 
-        views = {"ra": row_view(ra), "rb": row_view(rb_bytes), "h": row_view(h), "d": row_view(d), "x": row_view(x)}
-        rel_h_v, rel_x_v = row_view(rel_h), row_view(rel_x)
+        row_views = {name: by_row_tile(t) for name, t in (("ra", ra), ("rb", rb_bytes), ("h", h), ("d", d), ("x", x))}
+        rel_h_view, rel_x_view = by_row_tile(rel_h), by_row_tile(rel_x)
         rows = {}
 
         def load_rows(name, first, count):
-            view = views[name]
-            pool = xin if name == "x" else stream
-            t = pool.tile([P, count, view.shape[2]], view.dtype, name=name + "_in", align_bytes=64)
-            nc.sync.dma_start(out=t[:], in_=view[:, first : first + count, :])
+            view = row_views[name]
+            pool = stream_x if name == "x" else stream
+            tile = pool.tile([P, count, view.shape[2]], view.dtype, name=name + "_rows", align_bytes=64)
+            nc.sync.dma_start(out=tile[:], in_=view[:, first : first + count, :])
             for k in range(count):
-                rows[name, first + k] = t[:, k, :]
+                rows[name, first + k] = tile[:, k, :]
 
-        ident = keep.tile([P, P], F32, name="ident")
-        make_identity(nc, ident[:])
-        bsc = keep.tile([P, GB * N], U8, name="bsc", align_bytes=64)
-        usc = keep.tile([P, GN * D], U8, name="usc", align_bytes=64)
-        nc.vector.memset(bsc[:].bitcast(I32), 0)
-        nc.vector.memset(usc[:].bitcast(I32), 0)
+        identity = keep.tile([P, P], F32, name="identity")
+        make_identity(nc, identity[:])
+        b_scl = keep.tile([P, GB * N], U8, name="b_scl", align_bytes=64)
+        u_scl = keep.tile([P, GN * D], U8, name="u_scl", align_bytes=64)
+        nc.vector.memset(b_scl[:].bitcast(I32), 0)
+        nc.vector.memset(u_scl[:].bitcast(I32), 0)
         rb_scl = keep.tile([P, GB, 4], F32, name="rb_scl")
-        b_sb = [keep.tile([P, GB, 2 * COLS], U8, name=f"b_sb{k}", align_bytes=64) for k in range(2)]
+        b_sb = [keep.tile([P, GB, 2 * COLS], U8, name=f"b_sb{half}", align_bytes=64) for half in range(2)]
         u_sb = keep.tile([P, GN, 2 * D], U8, name="u_sb", align_bytes=64)
-        a_raw = {}
+        a_raw, a_grouped, a_codes, a_scl = {}, {}, {}, {}
 
         def load_a(g, half):
-            a_raw[g, half] = araw_pool.tile([P, 4, COLS], BF16, name="a_raw", align_bytes=64)
-            src = a[512 * g : 512 * (g + 1), COLS * half : COLS * (half + 1)]
-            nc.sync.dma_start(out=a_raw[g, half][:], in_=src.rearrange("(p j) n -> p j n", j=4))
+            a_raw[g, half] = a_raw_pool.tile([P, 4, COLS], BF16, name="a_raw", align_bytes=64)
+            block = a[PASS * g : PASS * (g + 1), COLS * half : COLS * (half + 1)]
+            nc.sync.dma_start(out=a_raw[g, half][:], in_=block.rearrange("(p t) n -> p t n", t=4))
 
         def load_b(half):
-            cols = slice(2 * COLS * half, 2 * COLS * (half + 1))
-            nc.sync.dma_start(out=b_sb[half][:], in_=b_words[:, :, cols].rearrange("g p c -> p g c"))
+            block = b_words[:, :, 2 * COLS * half : 2 * COLS * (half + 1)]
+            nc.sync.dma_start(out=b_sb[half][:], in_=block.rearrange("g p c -> p g c"))
 
-        def load_scales(tile, src, groups):
+        def load_scales(tile, scales, passes):
             for q in range(4):
                 nc.sync.dma_start(
-                    out=tile[32 * q : 32 * q + 4, :].bitcast(I32).rearrange("p (g n) -> p g n", g=groups),
-                    in_=src[:, 4 * q : 4 * q + 4, :].bitcast(I32).rearrange("g q n -> q g n"),
+                    out=tile[32 * q : 32 * q + 4, :].bitcast(I32).rearrange("p (g n) -> p g n", g=passes),
+                    in_=scales[:, 4 * q : 4 * q + 4, :].bitcast(I32).rearrange("g q n -> q g n"),
                 )
 
-        load_rows("rb", 0, 1)
-        nc.sync.dma_start(out=rb_scl[:], in_=rb_scale[0].rearrange("(g p t) -> p g t", g=GB, t=4))
-        load_scales(bsc, b_scales, GB)
-        load_a(1, 0)
-        load_a(0, 0)
-        load_b(0)
-        load_rows("ra", 0, 1)
-        load_a(0, 1)
-        load_a(1, 1)
-        load_rows("rb", 1, 1)
-        load_b(1)
-        load_rows("d", 0, 1)
-        load_rows("h", 0, 1)
-        load_rows("ra", 1, 1)
-        load_rows("rb", 2, 2)
-        load_rows("ra", 2, 2)
-        load_rows("d", 1, 1)
-        load_rows("h", 1, 1)
-        load_rows("rb", 4, 2)
-        load_rows("ra", 4, 2)
-        load_rows("d", 2, 2)
-        load_rows("h", 2, 2)
-        load_scales(usc, u_scales, GN)
-        nc.sync.dma_start(out=u_sb[:], in_=u_words.rearrange("g p c -> p g c"))
-        load_rows("x", 0, 2)
-        load_rows("d", 4, 2)
-        load_rows("h", 4, 2)
+        widened, permuted, banks, grouped, codes, scls = {}, {}, {}, {}, {}, {}
 
-        rbw, banks, grp, codes, scls, recip, sgn, f_sb = {}, {}, {}, {}, {}, {}, {}, {}
-        c_acc, x_acc, rel_t, ox_t = {}, {}, {}, {}
+        def keep_warm(count):
+            bank = turn_psum.tile([P, 2, 2, P], F32, name="bank")
+            for k in range(count):
+                nc.tensor.matmul(bank[:, 0, 0, :], lhsT=identity[:], rhs=identity[:], start=True, stop=True)
 
-        def widen(i, engine_copy):
-            rbw[i] = deep.tile([P, KB], BF16, name="rbw", align_bytes=64)
-            for k in range(1):
-                cols = slice(k * KB // 1, (k + 1) * KB // 1)
-                engine_copy(out=rbw[i][:, cols], in_=rows["rb", i][:, cols].bitcast(FP8))
-
-        def turn(words, base, step):
-            xt = t_psum.tile([P, 2, 2, P], F32, name="xt")
+        def turn(words, first_word):
+            bank = turn_psum.tile([P, 2, 2, P], F32, name="bank")
             for g in range(2):
                 for u in range(2):
-                    if step == 2:
-                        first = base + 256 * g + u
-                        src = words[:, first : first + 255 : 2]
-                    else:
-                        first = base + 256 * g + 128 * u
-                        src = words[:, first : first + 128]
-                    nc.tensor.transpose(xt[:, g, u, :], src, ident[:])
-            return xt
+                    nc.tensor.transpose(bank[:, g, u, :], first_word(words, g, u), identity[:])
+            return bank
 
-        def turn_and_group(kind, i, words, step):
-            xt = turn(words, 0, step)
-            grp[kind, i] = work.tile([P, 1024], BF16, name=kind + "_grp", align_bytes=64)
-            nc.scalar.copy(
-                out=grp[kind, i][:].bitcast(F32).rearrange("p (g r u) -> p g r u", g=2, u=2),
-                in_=xt[:].rearrange("p g u r -> p g r u"),
-            )
+        def every_second_word(words, g, u):
+            return words[:, 256 * g + u : 256 * g + 256 : 2]
 
-        def turn_ra(i):
-            turn_and_group("ra", i, rows["ra", i].bitcast(F32), 2)
+        def contiguous_words(words, g, u):
+            return words[:, 256 * g + 128 * u : 256 * g + 128 * (u + 1)]
 
-        def turn_f(i):
-            turn_and_group("f", i, f_sb[i][:].bitcast(F32), 1)
+        def widen_rb(i, copy):
+            widened[i] = ahead.tile([P, KB], BF16, name="widened", align_bytes=64)
+            copy(out=widened[i][:], in_=rows["rb", i].bitcast(E4M3))
 
         def turn_rb(i, half):
-            banks[half] = turn(rbw[i][:].bitcast(F32), 512 * half, 2)
+            banks["rb", i, half] = turn(widened[i][:, KB // 2 * half : KB // 2 * (half + 1)].bitcast(F32), every_second_word)
 
         def scale_rb(i, half):
             if half == 0:
-                grp["rb", i] = work.tile([P, KB], BF16, name="rb_grp", align_bytes=64)
-            bank = banks[half][:].rearrange("p g u r -> p (g u r)").bitcast(BF16)
+                grouped["rb", i] = work.tile([P, KB], BF16, name="rb_grouped", align_bytes=64)
+            bank = banks["rb", i, half][:].rearrange("p g u r -> p (g u r)").bitcast(BF16)
             for k in range(2):
                 g = 2 * half + k
                 nc.vector.tensor_tensor(
-                    out=grp["rb", i][:, 512 * g : 512 * (g + 1)].rearrange("p (r u e) -> p r u e", u=2, e=2),
-                    in0=bank[:, 512 * k : 512 * (k + 1)].rearrange("p (u r e) -> p r u e", u=2, e=2),
+                    out=grouped["rb", i][:, PASS * g : PASS * (g + 1)].rearrange("p (r u e) -> p r u e", u=2, e=2),
+                    in0=bank[:, PASS * k : PASS * (k + 1)].rearrange("p (u r e) -> p r u e", u=2, e=2),
                     in1=rb_scl[:, g, :].rearrange("p (o u e) -> p o u e", o=1, u=2).to_broadcast([P, P, 2, 2]),
                     op=ALU.mult,
                 )
 
-        def quant(kind, i):
-            width = grp[kind, i].shape[1]
-            codes[kind, i] = deep.tile([P, width // 4], U32, name=kind + "_codes", align_bytes=64)
-            scls[kind, i] = deep.tile([P, width // 4], U8, name=kind + "_scls", align_bytes=64)
-            nc.vector.quantize_mx(out=codes[kind, i][:].bitcast(FP8X4), scales=scls[kind, i][:], in_=grp[kind, i][:])
+        def permute_ra(i):
+            permuted[i] = work.tile([P, KA], BF16, name="permuted", align_bytes=64)
+            nc.scalar.copy(
+                out=permuted[i][:].bitcast(F32).rearrange("p (g u w) -> p g u w", g=GA, u=2),
+                in_=rows["ra", i].bitcast(F32).rearrange("p (g w u) -> p g u w", g=GA, u=2),
+            )
 
-        def reciprocal_d(i):
-            y = work.tile([P, N], F32, name="y")
-            nc.scalar.activation(out=y[:], in_=rows["d", i], func=ACT.Abs_reciprocal_sqrt)
-            nc.scalar.activation(out=y[:], in_=y[:], func=ACT.Square)
-            recip[i] = y
-            sgn[i] = work.tile([P, N], BF16, name="sgn")
+        def turn_ra(i):
+            if i in permuted:
+                banks["ra", i] = turn(permuted[i][:].bitcast(F32), contiguous_words)
+            else:
+                banks["ra", i] = turn(rows["ra", i].bitcast(F32), every_second_word)
+
+        def turn_f(i):
+            banks["f", i] = turn(f_rows[i][:].bitcast(F32), contiguous_words)
+
+        def group(kind, i):
+            grouped[kind, i] = work.tile([P, 2 * PASS], BF16, name=kind + "_grouped", align_bytes=64)
+            nc.scalar.copy(
+                out=grouped[kind, i][:].bitcast(F32).rearrange("p (g r u) -> p g r u", g=2, u=2),
+                in_=banks[kind, i][:].rearrange("p g u r -> p g r u"),
+            )
+
+        def quantise(kind, i):
+            width = grouped[kind, i].shape[1]
+            codes[kind, i] = ahead.tile([P, width // 4], U32, name=kind + "_codes", align_bytes=64)
+            scls[kind, i] = ahead.tile([P, width // 4], U8, name=kind + "_scl", align_bytes=64)
+            nc.vector.quantize_mx(
+                out=codes[kind, i][:].bitcast(E4M3X4), scales=scls[kind, i][:], in_=grouped[kind, i][:]
+            )
+
+        def gpsimd_copy(out, in_):
+            nc.gpsimd.tensor_scalar(out=out, in0=in_, scalar1=1.0, scalar2=0.0, op0=ALU.mult, op1=ALU.add)
+
+        def group_a(g, half, copy):
+            a_grouped[g, half] = a_grouped_pool.tile([P, COLS, 4], BF16, name="a_grouped", align_bytes=64)
+            copy(out=a_grouped[g, half][:], in_=a_raw[g, half][:].rearrange("p t n -> p n t"))
+
+        def quantise_a(g, half):
+            a_codes[g, half] = keep.tile([P, COLS], U32, name=f"a_codes{g}{half}", align_bytes=64)
+            a_scl[g, half] = keep.tile([P, COLS], U8, name=f"a_scl{g}{half}", align_bytes=64)
+            nc.vector.quantize_mx(
+                out=a_codes[g, half][:].bitcast(E4M3X4),
+                scales=a_scl[g, half][:],
+                in_=a_grouped[g, half][:].rearrange("p n t -> p (n t)"),
+            )
+
+        reciprocals, signs = {}, {}
+
+        def u_first(ap):
+            return ap.rearrange("p (w u e) -> p u w e", u=2, e=2)
+
+        def root_d(i):
+            reciprocals[i] = work.tile([P, N], F32, name="reciprocal")
+            nc.scalar.activation(out=reciprocals[i][:], in_=rows["d", i], func=ACT.Abs_reciprocal_sqrt)
+
+        def square_root_d(i):
+            nc.scalar.activation(out=reciprocals[i][:], in_=reciprocals[i][:], func=ACT.Square)
+
+        def sign_d(i):
+            signs[i] = work.tile([P, N], BF16, name="sign")
             for half in range(2):
                 cols = slice(COLS * half, COLS * (half + 1))
                 nc.scalar.activation(
-                    out=sgn[i][:, cols].rearrange("p (u w e) -> p u w e", u=2, e=2),
-                    in_=rows["d", i][:, cols].rearrange("p (w u e) -> p u w e", u=2, e=2),
+                    out=signs[i][:, cols].rearrange("p (u w e) -> p u w e", u=2, e=2),
+                    in_=u_first(rows["d", i][:, cols]),
                     func=ACT.Sign,
                 )
 
-        def signed(i, half):
-            cols = slice(COLS * half, COLS * (half + 1))
-            nc.vector.tensor_tensor(out=f_sb[i][:, cols], in0=f_sb[i][:, cols], in1=sgn[i][:, cols], op=ALU.mult)
+        c_banks, x_banks, rel_rows, f_rows, x_rows = {}, {}, {}, {}, {}
 
-        def mx(out, kind, i, g, moving, moving_scale, start, stop):
-            cols = slice(128 * g, 128 * (g + 1))
+        def mx_pass(bank, kind, i, g, moving, moving_scl, start, stop):
+            cols = slice(P * g, P * (g + 1))
             nc.tensor.matmul_mx(
-                out=out,
-                lhsT=codes[kind, i][:, cols].bitcast(FP8X4),
+                out=bank[:],
+                lhsT=codes[kind, i][:, cols].bitcast(E4M3X4),
                 lhsT_scale=scls[kind, i][:, cols],
                 rhs=moving,
-                rhs_scale=moving_scale,
+                rhs_scale=moving_scl,
                 start=start,
                 stop=stop,
             )
 
         def product_c(i, half):
-            acc = c_psum.tile([P, COLS], F32, name="c_acc")
-            c_acc[half] = acc
+            bank = c_psum.tile([P, COLS], F32, name="c_bank")
+            c_banks[i, half] = bank
             for g in range(GB):
-                moving = b_sb[half][:, g, :].bitcast(FP4X4)
-                scale = bsc[:, N * g + COLS * half : N * g + COLS * (half + 1)]
-                mx(acc[:], "rb", i, g, moving, scale, g == 0, False)
+                scl = b_scl[:, N * g + COLS * half : N * g + COLS * (half + 1)]
+                mx_pass(bank, "rb", i, g, b_sb[half][:, g, :].bitcast(E2M1X4), scl, g == 0, False)
             for g in range(GA):
-                mx(acc[:], "ra", i, g, a_codes[g, half][:].bitcast(FP8X4), a_scls[g, half][:], False, g == GA - 1)
+                moving = a_codes[g, half][:].bitcast(E4M3X4)
+                mx_pass(bank, "ra", i, g, moving, a_scl[g, half][:], False, g == GA - 1)
 
-        def relevance(i, half, engine):
+        def relevance(i, half):
             if half == 0:
-                rel_t[i] = outs.tile([P, N], F32, name="rel")
-                f_sb[i] = work.tile([P, N], BF16, name="f_sb")
+                rel_rows[i] = results.tile([P, N], F32, name="rel_rows")
             cols = slice(COLS * half, COLS * (half + 1))
-            nc.vector.tensor_tensor(out=rel_t[i][:, cols], in0=c_acc[half][:], in1=rows["h", i][:, cols], op=ALU.mult)
+            nc.vector.tensor_tensor(
+                out=rel_rows[i][:, cols], in0=c_banks[i, half][:], in1=rows["h", i][:, cols], op=ALU.mult
+            )
+
+        def ratio(i, half, engine):
+            if half == 0:
+                f_rows[i] = work.tile([P, N], BF16, name="f_rows")
+            cols = slice(COLS * half, COLS * (half + 1))
             engine.tensor_tensor(
-                out=f_sb[i][:, cols].rearrange("p (u w e) -> p u w e", u=2, e=2),
-                in0=rel_t[i][:, cols].rearrange("p (w u e) -> p u w e", u=2, e=2),
-                in1=recip[i][:, cols].rearrange("p (w u e) -> p u w e", u=2, e=2),
+                out=f_rows[i][:, cols].rearrange("p (u w e) -> p u w e", u=2, e=2),
+                in0=u_first(rel_rows[i][:, cols]),
+                in1=u_first(reciprocals[i][:, cols]),
                 op=ALU.mult,
             )
-            if half == 1:
-                nc.sync.dma_start(out=rel_h_v[:, i, :], in_=rel_t[i][:])
 
-        def back(i):
-            for c in range(3):
-                acc = b_psum.tile([P, COLS], F32, name="x_acc")
-                for g in range(GN):
-                    moving = u_sb[:, g, 2 * COLS * c : 2 * COLS * (c + 1)].bitcast(FP4X4)
-                    scale = usc[:, D * g + COLS * c : D * g + COLS * (c + 1)]
-                    mx(acc[:], "f", i, g, moving, scale, g == 0, g == GN - 1)
-                x_acc[i, c] = acc
-
-        def finish(i):
-            ox_t[i] = outs.tile([P, D], F32, name="ox")
-            for c in range(3):
-                cols = slice(COLS * c, COLS * (c + 1))
-                nc.vector.tensor_tensor(out=ox_t[i][:, cols], in0=x_acc[i, c][:], in1=rows["x", i][:, cols], op=ALU.mult)
-                if i == TILES - 1:
-                    nc.sync.dma_start(out=rel_x_v[:, i, cols], in_=ox_t[i][:, cols])
-            if i < TILES - 1:
-                nc.sync.dma_start(out=rel_x_v[:, i, :], in_=ox_t[i][:])
-
-        a_grp, a_codes, a_scls = {}, {}, {}
-
-        def gpsimd_copy(out, in_):
-            nc.gpsimd.tensor_scalar(out=out, in0=in_, scalar1=1.0, scalar2=0.0, op0=ALU.mult, op1=ALU.add)
-
-        def group_a(engine_copy, g, half):
-            a_grp[g, half] = agrp_pool.tile([P, COLS, 4], BF16, name="a_grp", align_bytes=64)
-            engine_copy(out=a_grp[g, half][:], in_=a_raw[g, half][:].rearrange("p j n -> p n j"))
-
-        def quant_a(g, half):
-            a_codes[g, half] = keep.tile([P, COLS], U32, name=f"a_codes{g}{half}", align_bytes=64)
-            a_scls[g, half] = keep.tile([P, COLS], U8, name=f"a_scls{g}{half}", align_bytes=64)
-            nc.vector.quantize_mx(
-                out=a_codes[g, half][:].bitcast(FP8X4),
-                scales=a_scls[g, half][:],
-                in_=a_grp[g, half][:].rearrange("p n j -> p (n j)"),
+        def apply_sign(i, half):
+            cols = slice(COLS * half, COLS * (half + 1))
+            nc.vector.tensor_tensor(
+                out=f_rows[i][:, cols], in0=f_rows[i][:, cols], in1=signs[i][:, cols], op=ALU.mult
             )
 
-        widen(0, nc.vector.tensor_copy)
-        turn_rb(0, 0)
-        turn_rb(0, 1)
-        group_a(nc.scalar.copy, 0, 0)
-        scale_rb(0, 0)
-        group_a(gpsimd_copy, 1, 0)
-        scale_rb(0, 1)
+        def store_rel_h(i):
+            nc.sync.dma_start(out=rel_h_view[:, i, :], in_=rel_rows[i][:])
+
+        def product_x(i):
+            for c in range(X_CHUNKS):
+                x_banks[i, c] = x_psum.tile([P, COLS], F32, name="x_bank")
+                for g in range(GN):
+                    moving = u_sb[:, g, 2 * COLS * c : 2 * COLS * (c + 1)].bitcast(E2M1X4)
+                    scl = u_scl[:, D * g + COLS * c : D * g + COLS * (c + 1)]
+                    mx_pass(x_banks[i, c], "f", i, g, moving, scl, g == 0, g == GN - 1)
+
+        def finish(i, c):
+            if c == 0:
+                x_rows[i] = results.tile([P, D], F32, name="x_rows")
+            cols = slice(COLS * c, COLS * (c + 1))
+            nc.vector.tensor_tensor(
+                out=x_rows[i][:, cols], in0=x_banks[i, c][:], in1=rows["x", i][:, cols], op=ALU.mult
+            )
+            if i == LAST:
+                nc.sync.dma_start(out=rel_x_view[:, i, cols], in_=x_rows[i][:, cols])
+            elif c == X_CHUNKS - 1:
+                nc.sync.dma_start(out=rel_x_view[:, i, :], in_=x_rows[i][:])
+
+        load_rows("rb", 0, 1)
+        load_rows("ra", 0, 1)
+        nc.sync.dma_start(out=rb_scl[:], in_=rb_scale[0].rearrange("(g p t) -> p g t", g=GB, t=4))
+        load_rows("rb", 1, 1)
+        load_rows("d", 0, 1)
+        load_a(1, 0)
+        load_scales(b_scl, b_scales, GB)
+        load_a(0, 0)
+        load_rows("ra", 1, 1)
+        load_b(0)
+        load_rows("rb", 2, 2)
+        load_a(0, 1)
+        load_a(1, 1)
+        load_rows("h", 0, 1)
+        load_rows("d", 1, 1)
+        load_b(1)
+        load_rows("ra", 2, 2)
+        load_rows("h", 1, 1)
+        load_scales(u_scl, u_scales, GN)
+        nc.sync.dma_start(out=u_sb[:], in_=u_words.rearrange("g p c -> p g c"))
+        load_rows("d", 2, 2)
+        load_rows("h", 2, 2)
+        load_rows("ra", 4, 2)
+        load_rows("rb", 4, 2)
+        load_rows("x", 0, 2)
+        load_rows("d", 4, 2)
+        load_rows("h", 4, 2)
+
+        keep_warm(4)
+        widen_rb(0, nc.vector.tensor_copy)
+        widen_rb(1, nc.vector.tensor_copy)
+        group_a(1, 0, gpsimd_copy)
         turn_ra(0)
-        quant("rb", 0)
-        quant_a(0, 0)
-        quant("ra", 0)
-        quant_a(1, 0)
-        product_c(0, 0)
-        group_a(nc.scalar.copy, 0, 1)
-        group_a(nc.vector.tensor_copy, 1, 1)
-        widen(1, nc.vector.tensor_copy)
+        group("ra", 0)
+        sign_d(0)
+        root_d(0)
+        group_a(0, 0, nc.scalar.copy)
+        turn_rb(0, 0)
+        scale_rb(0, 0)
+        turn_rb(0, 1)
+        scale_rb(0, 1)
         turn_rb(1, 0)
-        turn_rb(1, 1)
-        turn_ra(1)
-        quant_a(0, 1)
-        quant_a(1, 1)
-        reciprocal_d(0)
-        relevance(0, 0, nc.gpsimd)
         scale_rb(1, 0)
+        turn_rb(1, 1)
+        keep_warm(1)
+        turn_ra(1)
+        keep_warm(2)
+        quantise("ra", 0)
+        quantise("rb", 0)
         scale_rb(1, 1)
-        quant("ra", 1)
-        product_c(0, 1)
-        quant("rb", 1)
-        widen(2, nc.vector.tensor_copy)
-        relevance(0, 1, nc.gpsimd)
-        turn_ra(2)
+        quantise_a(0, 0)
+        quantise_a(1, 0)
+        product_c(0, 0)
+        group("ra", 1)
+        square_root_d(0)
+        quantise("ra", 1)
+        quantise("rb", 1)
+        widen_rb(2, nc.vector.tensor_copy)
+        group_a(0, 1, nc.scalar.copy)
+        group_a(1, 1, nc.vector.tensor_copy)
+        quantise_a(0, 1)
+        quantise_a(1, 1)
         turn_rb(2, 0)
-        scale_rb(2, 0)
         turn_rb(2, 1)
+        product_c(0, 1)
+        root_d(1)
+        sign_d(1)
+        permute_ra(2)
+        turn_ra(2)
+        square_root_d(1)
+        relevance(0, 0)
+        ratio(0, 0, nc.gpsimd)
+        scale_rb(2, 0)
+        relevance(0, 1)
+        ratio(0, 1, nc.gpsimd)
+        apply_sign(0, 0)
         scale_rb(2, 1)
-        quant("ra", 2)
-        quant("rb", 2)
-        reciprocal_d(1)
-        signed(0, 0)
-        signed(0, 1)
-        widen(3, nc.scalar.copy)
+        group("ra", 2)
+        widen_rb(3, nc.scalar.copy)
+        apply_sign(0, 1)
+        quantise("ra", 2)
+        quantise("rb", 2)
         load_rows("rb", 6, 2)
+        store_rel_h(0)
         load_rows("ra", 6, 2)
 
         for s in range(1, TILES):
-            last = s == TILES - 1
+            ratio_engine = nc.vector if s == LAST else nc.gpsimd
+            if s >= 2:
+                finish(s - 2, 0)
+                finish(s - 2, 1)
+            if s + 2 < TILES:
+                permute_ra(s + 2)
             product_c(s, 0)
-            relevance(s, 0, nc.vector if last else nc.gpsimd)
-            if s >= 2 and not last:
-                finish(s - 2)
+            relevance(s, 0)
+            ratio(s, 0, ratio_engine)
+            if s >= 2:
+                finish(s - 2, 2)
             turn_f(s - 1)
-            if s + 2 < TILES:
-                turn_ra(s + 2)
-            quant("f", s - 1)
-            if last:
-                finish(s - 2)
-            if s + 2 < TILES:
-                quant("ra", s + 2)
-            product_c(s, 1)
-            relevance(s, 1, nc.vector if last else nc.gpsimd)
-            if s + 3 < TILES:
-                widen(s + 3, nc.scalar.copy)
-            if s + 1 < TILES:
-                reciprocal_d(s + 1)
+            group("f", s - 1)
             if s + 2 < TILES:
                 turn_rb(s + 2, 0)
+                turn_ra(s + 2)
+            if s + 1 < TILES:
+                root_d(s + 1)
+            if s + 2 < TILES:
+                group("ra", s + 2)
+            if s + 1 < TILES:
+                sign_d(s + 1)
+            if s + 3 < TILES:
+                widen_rb(s + 3, nc.scalar.copy)
+            if s + 1 < TILES:
+                square_root_d(s + 1)
+            if s + 2 < TILES:
                 scale_rb(s + 2, 0)
+            quantise("f", s - 1)
+            apply_sign(s, 0)
+            if s + 2 < TILES:
+                quantise("ra", s + 2)
+            product_c(s, 1)
+            relevance(s, 1)
+            ratio(s, 1, ratio_engine)
+            store_rel_h(s)
+            if s + 2 < TILES:
                 turn_rb(s + 2, 1)
                 scale_rb(s + 2, 1)
-                quant("rb", s + 2)
-            signed(s, 0)
-            signed(s, 1)
-            back(s - 1)
+                quantise("rb", s + 2)
+            apply_sign(s, 1)
+            product_x(s - 1)
             if s == 1:
                 load_rows("x", 2, 2)
                 load_rows("d", 6, 2)
@@ -343,8 +404,13 @@ def tile_relevance_step_fanout_s3_kernel(
                 load_rows("x", 4, 2)
             if s == 4:
                 load_rows("x", 6, 2)
-        turn_f(TILES - 1)
-        finish(TILES - 2)
-        quant("f", TILES - 1)
-        back(TILES - 1)
-        finish(TILES - 1)
+
+        turn_f(LAST)
+        group("f", LAST)
+        for c in range(X_CHUNKS):
+            finish(LAST - 1, c)
+        quantise("f", LAST)
+        keep_warm(2)
+        product_x(LAST)
+        for c in range(X_CHUNKS):
+            finish(LAST, c)

from contextlib import ExitStack

import concourse.mybir as mybir
from concourse.masks import make_identity

M, KA, KB, N, D = 1024, 1024, 2048, 1024, 1536
FLOPS = 2 * M * (KA * N + KB * N + N * D)

F32 = mybir.dt.float32
BF16 = mybir.dt.bfloat16
I32 = mybir.dt.int32
U32 = mybir.dt.uint32
U8 = mybir.dt.uint8
E4M3 = mybir.dt.float8_e4m3fn
E4M3X4 = mybir.dt.float8_e4m3fn_x4
E2M1X4 = mybir.dt.float4_e2m1fn_x4
ALU = mybir.AluOpType
ACT = mybir.ActivationFunctionType

P = 128
TILES = M // P
PASS = 512
COLS = 512
GA, GB, GN = KA // PASS, KB // PASS, N // PASS
X_CHUNKS = D // COLS
LAST = TILES - 1


def tile_relevance_step_fanout_s3_kernel(
    tc, ra, a, rb_bytes, rb_scale, b_words, b_scales, h, d, x, u_words, u_scales, rel_h, rel_x
):
    nc = tc.nc
    with ExitStack() as ctx:
        keep = ctx.enter_context(tc.tile_pool(name="keep", bufs=1))
        stream = ctx.enter_context(tc.tile_pool(name="stream", bufs=4))
        stream_x = ctx.enter_context(tc.tile_pool(name="stream_x", bufs=3))
        a_raw_pool = ctx.enter_context(tc.tile_pool(name="a_raw", bufs=4))
        a_grouped_pool = ctx.enter_context(tc.tile_pool(name="a_grouped", bufs=2))
        work = ctx.enter_context(tc.tile_pool(name="work", bufs=2))
        ahead = ctx.enter_context(tc.tile_pool(name="ahead", bufs=3))
        results = ctx.enter_context(tc.tile_pool(name="results", bufs=3))
        c_psum = ctx.enter_context(tc.psum_pool(name="c_psum", bufs=2))
        x_psum = ctx.enter_context(tc.psum_pool(name="x_psum", bufs=3))
        turn_psum = ctx.enter_context(tc.psum_pool(name="turn_psum", bufs=3))
        ctx.enter_context(tc.manual_schedule())

        def by_row_tile(tensor):
            return tensor.rearrange("(p i) k -> p i k", i=TILES)

        row_views = {name: by_row_tile(t) for name, t in (("ra", ra), ("rb", rb_bytes), ("h", h), ("d", d), ("x", x))}
        rel_h_view, rel_x_view = by_row_tile(rel_h), by_row_tile(rel_x)
        rows = {}

        def load_rows(name, first, count):
            view = row_views[name]
            pool = stream_x if name == "x" else stream
            tile = pool.tile([P, count, view.shape[2]], view.dtype, name=name + "_rows", align_bytes=64)
            nc.sync.dma_start(out=tile[:], in_=view[:, first : first + count, :])
            for k in range(count):
                rows[name, first + k] = tile[:, k, :]

        identity = keep.tile([P, P], F32, name="identity")
        make_identity(nc, identity[:])
        b_scl = keep.tile([P, GB * N], U8, name="b_scl", align_bytes=64)
        u_scl = keep.tile([P, GN * D], U8, name="u_scl", align_bytes=64)
        nc.vector.memset(b_scl[:].bitcast(I32), 0)
        nc.vector.memset(u_scl[:].bitcast(I32), 0)
        rb_scl = keep.tile([P, GB, 4], F32, name="rb_scl")
        b_sb = [keep.tile([P, GB, 2 * COLS], U8, name=f"b_sb{half}", align_bytes=64) for half in range(2)]
        u_sb = keep.tile([P, GN, 2 * D], U8, name="u_sb", align_bytes=64)
        a_raw, a_grouped, a_codes, a_scl = {}, {}, {}, {}

        def load_a(g, half):
            a_raw[g, half] = a_raw_pool.tile([P, 4, COLS], BF16, name="a_raw", align_bytes=64)
            block = a[PASS * g : PASS * (g + 1), COLS * half : COLS * (half + 1)]
            nc.sync.dma_start(out=a_raw[g, half][:], in_=block.rearrange("(p t) n -> p t n", t=4))

        def load_b(half):
            block = b_words[:, :, 2 * COLS * half : 2 * COLS * (half + 1)]
            nc.sync.dma_start(out=b_sb[half][:], in_=block.rearrange("g p c -> p g c"))

        def load_scales(tile, scales, passes):
            for q in range(4):
                nc.sync.dma_start(
                    out=tile[32 * q : 32 * q + 4, :].bitcast(I32).rearrange("p (g n) -> p g n", g=passes),
                    in_=scales[:, 4 * q : 4 * q + 4, :].bitcast(I32).rearrange("g q n -> q g n"),
                )

        widened, permuted, banks, grouped, codes, scls = {}, {}, {}, {}, {}, {}

        def keep_warm(count):
            bank = turn_psum.tile([P, 2, 2, P], F32, name="bank")
            for k in range(count):
                nc.tensor.matmul(bank[:, 0, 0, :], lhsT=identity[:], rhs=identity[:], start=True, stop=True)

        def turn(words, first_word):
            bank = turn_psum.tile([P, 2, 2, P], F32, name="bank")
            for g in range(2):
                for u in range(2):
                    nc.tensor.transpose(bank[:, g, u, :], first_word(words, g, u), identity[:])
            return bank

        def every_second_word(words, g, u):
            return words[:, 256 * g + u : 256 * g + 256 : 2]

        def contiguous_words(words, g, u):
            return words[:, 256 * g + 128 * u : 256 * g + 128 * (u + 1)]

        def widen_rb(i, copy):
            widened[i] = ahead.tile([P, KB], BF16, name="widened", align_bytes=64)
            copy(out=widened[i][:], in_=rows["rb", i].bitcast(E4M3))

        def turn_rb(i, half):
            banks["rb", i, half] = turn(widened[i][:, KB // 2 * half : KB // 2 * (half + 1)].bitcast(F32), every_second_word)

        def scale_rb(i, half):
            if half == 0:
                grouped["rb", i] = work.tile([P, KB], BF16, name="rb_grouped", align_bytes=64)
            bank = banks["rb", i, half][:].rearrange("p g u r -> p (g u r)").bitcast(BF16)
            for k in range(2):
                g = 2 * half + k
                nc.vector.tensor_tensor(
                    out=grouped["rb", i][:, PASS * g : PASS * (g + 1)].rearrange("p (r u e) -> p r u e", u=2, e=2),
                    in0=bank[:, PASS * k : PASS * (k + 1)].rearrange("p (u r e) -> p r u e", u=2, e=2),
                    in1=rb_scl[:, g, :].rearrange("p (o u e) -> p o u e", o=1, u=2).to_broadcast([P, P, 2, 2]),
                    op=ALU.mult,
                )

        def permute_ra(i):
            permuted[i] = work.tile([P, KA], BF16, name="permuted", align_bytes=64)
            nc.scalar.copy(
                out=permuted[i][:].bitcast(F32).rearrange("p (g u w) -> p g u w", g=GA, u=2),
                in_=rows["ra", i].bitcast(F32).rearrange("p (g w u) -> p g u w", g=GA, u=2),
            )

        def turn_ra(i):
            if i in permuted:
                banks["ra", i] = turn(permuted[i][:].bitcast(F32), contiguous_words)
            else:
                banks["ra", i] = turn(rows["ra", i].bitcast(F32), every_second_word)

        def turn_f(i):
            banks["f", i] = turn(f_rows[i][:].bitcast(F32), contiguous_words)

        def group(kind, i):
            grouped[kind, i] = work.tile([P, 2 * PASS], BF16, name=kind + "_grouped", align_bytes=64)
            nc.scalar.copy(
                out=grouped[kind, i][:].bitcast(F32).rearrange("p (g r u) -> p g r u", g=2, u=2),
                in_=banks[kind, i][:].rearrange("p g u r -> p g r u"),
            )

        def quantise(kind, i):
            width = grouped[kind, i].shape[1]
            codes[kind, i] = ahead.tile([P, width // 4], U32, name=kind + "_codes", align_bytes=64)
            scls[kind, i] = ahead.tile([P, width // 4], U8, name=kind + "_scl", align_bytes=64)
            nc.vector.quantize_mx(
                out=codes[kind, i][:].bitcast(E4M3X4), scales=scls[kind, i][:], in_=grouped[kind, i][:]
            )

        def gpsimd_copy(out, in_):
            nc.gpsimd.tensor_scalar(out=out, in0=in_, scalar1=1.0, scalar2=0.0, op0=ALU.mult, op1=ALU.add)

        def group_a(g, half, copy):
            a_grouped[g, half] = a_grouped_pool.tile([P, COLS, 4], BF16, name="a_grouped", align_bytes=64)
            copy(out=a_grouped[g, half][:], in_=a_raw[g, half][:].rearrange("p t n -> p n t"))

        def quantise_a(g, half):
            a_codes[g, half] = keep.tile([P, COLS], U32, name=f"a_codes{g}{half}", align_bytes=64)
            a_scl[g, half] = keep.tile([P, COLS], U8, name=f"a_scl{g}{half}", align_bytes=64)
            nc.vector.quantize_mx(
                out=a_codes[g, half][:].bitcast(E4M3X4),
                scales=a_scl[g, half][:],
                in_=a_grouped[g, half][:].rearrange("p n t -> p (n t)"),
            )

        reciprocals, signs = {}, {}

        def u_first(ap):
            return ap.rearrange("p (w u e) -> p u w e", u=2, e=2)

        def root_d(i):
            reciprocals[i] = work.tile([P, N], F32, name="reciprocal")
            nc.scalar.activation(out=reciprocals[i][:], in_=rows["d", i], func=ACT.Abs_reciprocal_sqrt)

        def square_root_d(i):
            nc.scalar.activation(out=reciprocals[i][:], in_=reciprocals[i][:], func=ACT.Square)

        def sign_d(i):
            signs[i] = work.tile([P, N], BF16, name="sign")
            for half in range(2):
                cols = slice(COLS * half, COLS * (half + 1))
                nc.scalar.activation(
                    out=signs[i][:, cols].rearrange("p (u w e) -> p u w e", u=2, e=2),
                    in_=u_first(rows["d", i][:, cols]),
                    func=ACT.Sign,
                )

        c_banks, x_banks, rel_rows, f_rows, x_rows = {}, {}, {}, {}, {}

        def mx_pass(bank, kind, i, g, moving, moving_scl, start, stop):
            cols = slice(P * g, P * (g + 1))
            nc.tensor.matmul_mx(
                out=bank[:],
                lhsT=codes[kind, i][:, cols].bitcast(E4M3X4),
                lhsT_scale=scls[kind, i][:, cols],
                rhs=moving,
                rhs_scale=moving_scl,
                start=start,
                stop=stop,
            )

        def product_c(i, half):
            bank = c_psum.tile([P, COLS], F32, name="c_bank")
            c_banks[i, half] = bank
            for g in range(GB):
                scl = b_scl[:, N * g + COLS * half : N * g + COLS * (half + 1)]
                mx_pass(bank, "rb", i, g, b_sb[half][:, g, :].bitcast(E2M1X4), scl, g == 0, False)
            for g in range(GA):
                moving = a_codes[g, half][:].bitcast(E4M3X4)
                mx_pass(bank, "ra", i, g, moving, a_scl[g, half][:], False, g == GA - 1)

        def relevance(i, half):
            if half == 0:
                rel_rows[i] = results.tile([P, N], F32, name="rel_rows")
            cols = slice(COLS * half, COLS * (half + 1))
            nc.vector.tensor_tensor(
                out=rel_rows[i][:, cols], in0=c_banks[i, half][:], in1=rows["h", i][:, cols], op=ALU.mult
            )

        def ratio(i, half, engine):
            if half == 0:
                f_rows[i] = work.tile([P, N], BF16, name="f_rows")
            cols = slice(COLS * half, COLS * (half + 1))
            engine.tensor_tensor(
                out=f_rows[i][:, cols].rearrange("p (u w e) -> p u w e", u=2, e=2),
                in0=u_first(rel_rows[i][:, cols]),
                in1=u_first(reciprocals[i][:, cols]),
                op=ALU.mult,
            )

        def apply_sign(i, half):
            cols = slice(COLS * half, COLS * (half + 1))
            nc.vector.tensor_tensor(
                out=f_rows[i][:, cols], in0=f_rows[i][:, cols], in1=signs[i][:, cols], op=ALU.mult
            )

        def store_rel_h(i):
            nc.sync.dma_start(out=rel_h_view[:, i, :], in_=rel_rows[i][:])

        def product_x(i):
            for c in range(X_CHUNKS):
                x_banks[i, c] = x_psum.tile([P, COLS], F32, name="x_bank")
                for g in range(GN):
                    moving = u_sb[:, g, 2 * COLS * c : 2 * COLS * (c + 1)].bitcast(E2M1X4)
                    scl = u_scl[:, D * g + COLS * c : D * g + COLS * (c + 1)]
                    mx_pass(x_banks[i, c], "f", i, g, moving, scl, g == 0, g == GN - 1)

        def finish(i, c):
            if c == 0:
                x_rows[i] = results.tile([P, D], F32, name="x_rows")
            cols = slice(COLS * c, COLS * (c + 1))
            nc.vector.tensor_tensor(
                out=x_rows[i][:, cols], in0=x_banks[i, c][:], in1=rows["x", i][:, cols], op=ALU.mult
            )
            if i == LAST:
                nc.sync.dma_start(out=rel_x_view[:, i, cols], in_=x_rows[i][:, cols])
            elif c == X_CHUNKS - 1:
                nc.sync.dma_start(out=rel_x_view[:, i, :], in_=x_rows[i][:])

        load_rows("rb", 0, 1)
        load_rows("ra", 0, 1)
        nc.sync.dma_start(out=rb_scl[:], in_=rb_scale[0].rearrange("(g p t) -> p g t", g=GB, t=4))
        load_rows("rb", 1, 1)
        load_rows("d", 0, 1)
        load_a(1, 0)
        load_scales(b_scl, b_scales, GB)
        load_a(0, 0)
        load_rows("ra", 1, 1)
        load_b(0)
        load_rows("rb", 2, 2)
        load_a(0, 1)
        load_a(1, 1)
        load_rows("h", 0, 1)
        load_rows("d", 1, 1)
        load_b(1)
        load_rows("ra", 2, 2)
        load_rows("h", 1, 1)
        load_scales(u_scl, u_scales, GN)
        nc.sync.dma_start(out=u_sb[:], in_=u_words.rearrange("g p c -> p g c"))
        load_rows("d", 2, 2)
        load_rows("h", 2, 2)
        load_rows("ra", 4, 2)
        load_rows("rb", 4, 2)
        load_rows("x", 0, 2)
        load_rows("d", 4, 2)
        load_rows("h", 4, 2)

        keep_warm(4)
        widen_rb(0, nc.vector.tensor_copy)
        widen_rb(1, nc.vector.tensor_copy)
        group_a(1, 0, gpsimd_copy)
        turn_ra(0)
        group("ra", 0)
        sign_d(0)
        root_d(0)
        group_a(0, 0, nc.scalar.copy)
        turn_rb(0, 0)
        scale_rb(0, 0)
        turn_rb(0, 1)
        scale_rb(0, 1)
        turn_rb(1, 0)
        scale_rb(1, 0)
        turn_rb(1, 1)
        keep_warm(1)
        turn_ra(1)
        keep_warm(2)
        quantise("ra", 0)
        quantise("rb", 0)
        scale_rb(1, 1)
        quantise_a(0, 0)
        quantise_a(1, 0)
        product_c(0, 0)
        group("ra", 1)
        square_root_d(0)
        quantise("ra", 1)
        quantise("rb", 1)
        widen_rb(2, nc.vector.tensor_copy)
        group_a(0, 1, nc.scalar.copy)
        group_a(1, 1, nc.vector.tensor_copy)
        quantise_a(0, 1)
        quantise_a(1, 1)
        turn_rb(2, 0)
        turn_rb(2, 1)
        product_c(0, 1)
        root_d(1)
        sign_d(1)
        permute_ra(2)
        turn_ra(2)
        square_root_d(1)
        relevance(0, 0)
        ratio(0, 0, nc.gpsimd)
        scale_rb(2, 0)
        relevance(0, 1)
        ratio(0, 1, nc.gpsimd)
        apply_sign(0, 0)
        scale_rb(2, 1)
        group("ra", 2)
        widen_rb(3, nc.scalar.copy)
        apply_sign(0, 1)
        quantise("ra", 2)
        quantise("rb", 2)
        load_rows("rb", 6, 2)
        store_rel_h(0)
        load_rows("ra", 6, 2)

        for s in range(1, TILES):
            ratio_engine = nc.vector if s == LAST else nc.gpsimd
            if s >= 2:
                finish(s - 2, 0)
                finish(s - 2, 1)
            if s + 2 < TILES:
                permute_ra(s + 2)
            product_c(s, 0)
            relevance(s, 0)
            ratio(s, 0, ratio_engine)
            if s >= 2:
                finish(s - 2, 2)
            turn_f(s - 1)
            group("f", s - 1)
            if s + 2 < TILES:
                turn_rb(s + 2, 0)
                turn_ra(s + 2)
            if s + 1 < TILES:
                root_d(s + 1)
            if s + 2 < TILES:
                group("ra", s + 2)
            if s + 1 < TILES:
                sign_d(s + 1)
            if s + 3 < TILES:
                widen_rb(s + 3, nc.scalar.copy)
            if s + 1 < TILES:
                square_root_d(s + 1)
            if s + 2 < TILES:
                scale_rb(s + 2, 0)
            quantise("f", s - 1)
            apply_sign(s, 0)
            if s + 2 < TILES:
                quantise("ra", s + 2)
            product_c(s, 1)
            relevance(s, 1)
            ratio(s, 1, ratio_engine)
            store_rel_h(s)
            if s + 2 < TILES:
                turn_rb(s + 2, 1)
                scale_rb(s + 2, 1)
                quantise("rb", s + 2)
            apply_sign(s, 1)
            product_x(s - 1)
            if s == 1:
                load_rows("x", 2, 2)
                load_rows("d", 6, 2)
                load_rows("h", 6, 2)
            if s == 2:
                load_rows("x", 4, 2)
            if s == 4:
                load_rows("x", 6, 2)

        turn_f(LAST)
        group("f", LAST)
        for c in range(X_CHUNKS):
            finish(LAST - 1, c)
        quantise("f", LAST)
        keep_warm(2)
        product_x(LAST)
        for c in range(X_CHUNKS):
            finish(LAST, c)
